import numpy as np, ml_dtypes
CORES = [23,119,17,113]
N = 4
BF = ml_dtypes.bfloat16
def gentries(a):
    return np.ascontiguousarray(a.reshape(8, 16, -1).transpose(0, 2, 1)).reshape(8, -1)
def gtable(e):
    e = np.asarray(e); return np.ascontiguousarray(e.reshape(8, -1, 16).transpose(0, 2, 1)).reshape(128, -1).astype(np.int32)
W, NB, P, Q, RO, ST, LO, HI, OWN = 8192, 512, 256, 32, 5, 1, 4, 9, 0
def sites(rng):
    b = np.argsort(rng.random((N, 8, NB)), axis=-1); o = np.argsort(rng.random((N, 8, NB)), axis=-1)
    return b, np.ascontiguousarray(o[..., :P]), np.take_along_axis(b, o[..., P:], -1)
def some(rng):
    x = rng.integers(0, 256, (N, 8, 16, W), dtype=np.int16); c = rng.integers(0, W, (N, 8, 16, NB))
    pf = rng.integers(0, 256, (N, 8, 16, P)); pn = rng.integers(0, 256, (N, 8, 16, P))
    th = (rng.choice(np.array([1, 60, 400]), (N, 8, 1)) * rng.random((N, 8, 16))).astype(np.int64)
    return x, c, pf, pn, th
def lay(b, fl, nu, ca, ch):
    c = np.zeros((N, 8, 16, NB), np.int64); a = np.take_along_axis(b, fl, -1)
    np.put_along_axis(c, a[:, :, None, :], ca, 3); np.put_along_axis(c, nu[:, :, None, :], ch, 3)
    return c
def pack(x, c, b, fl, nu, pf, pn, th):
    return {"xf": x.reshape(N, 128, W).astype(np.float32).astype(BF), "cb": np.ascontiguousarray(c.reshape(N, 128, NB)).astype(np.int32), "bs": np.stack([gtable(v) for v in b]),
            "fs": np.stack([gtable(v) for v in fl]), "nb": np.stack([gtable(v) for v in nu]), "pf": pf.reshape(N, 128, P).astype(np.float32).astype(BF),
            "pn": pn.reshape(N, 128, P).astype(np.float32).astype(BF), "th": np.ascontiguousarray(th.reshape(N, 128, 1)).astype(np.int32)}
def setup_inputs(rng):
    b, fl, nu = sites(rng); x, c, pf, pn, th = some(rng)
    return pack(x, c, b, fl, nu, pf, pn, th)
def setup_inputs_corners(rng):
    b, fl, nu = sites(rng)
    for q in range(N):
        for g in range(8):
            if g in (0, 3): b[q, g] = np.arange(NB)
            if g == 1: b[q, g] = np.arange(NB)[::-1]
            o = np.concatenate([fl[q, g], np.setdiff1d(np.arange(NB), fl[q, g])])
            if g == 2: o = np.concatenate([np.arange(0, NB, 2), rng.permutation(np.arange(1, NB, 2))])
            if g == 3: o = np.arange(NB)
            if g == 4: o = np.arange(NB)[::-1]
            if g == 5: o = np.concatenate([rng.permutation(P), P + rng.permutation(P)])
            fl[q, g] = o[:P]; nu[q, g] = b[q, g][o[P:]]
    order = np.argsort(rng.random((N, 8, W)), axis=-1)
    order[:, 6:] = order[0, 6:].copy()
    tot = np.concatenate([np.broadcast_to(np.arange(4081), (N, 8, 4081)), rng.integers(0, 4081, (N, 8, W - 4081))], axis=2)
    sg = np.zeros((N, 8, W), np.int64); np.put_along_axis(sg, order, tot, 2); sg = sg[:, :, None, :]
    ln = (np.arange(16)[:, None] + np.arange(W)[None, :]) % 16
    x = (sg // 16 + (ln[None, None] < sg % 16)).astype(np.int16); loc = order[:, :, None, :4081]
    th = rng.choice(np.array([0, 1, 2, 7, 300, 1001, 4095, 4096, 6001, 8158, 8159]), (N, 8, 16)); th[:, 6:] = rng.integers(1002, 4160, (N, 2, 16))
    want = rng.choice(np.array([0, LO, LO + 1, HI - 1, HI, 16]), (N, 8, P))
    for q in range(N):
        for g in range(8):
            m = (g + q) % 8
            if m < 4: want[q, g] = rng.choice(np.array(((HI, 16), (0, LO), (LO + 1, HI - 1), (16, 16))[m]), P)
    sw = np.argsort(np.argsort(rng.random((N, 8, 16, P)), axis=2), axis=2) < want[:, :, None, :]
    d = th[..., None] // 2 + sw; lo = (rng.random((N, 8, 16, P)) * (4081 - d)).astype(np.int64)
    ch = np.take_along_axis(loc, lo + d, 3); cl = np.take_along_axis(loc, lo, 3)
    u = rng.integers(0, 2, (N, 8, 1, P)); z = np.zeros((N, 8, 16, P), np.int64)
    ca = np.where(u == 0, ch, cl); cc = np.where(u == 0, cl, ch)
    mv = rng.random(P) < 0.5; mv[0] = True; mv[P - 1] = False
    u[:, 6, 0] = np.where(mv, rng.integers(0, 2, P), np.arange(N)[:, None] % 2); u[:, 7] = rng.integers(0, 2)
    for g in (6, 7):
        small, large = [w[(w & (min(Q, 16) - 1)) > 0] for w in (order[0, g, :1001], order[0, g, 3080:4081])]
        small = rng.choice(small, (N, 16, P)); large = rng.choice(large, (N, 16, P)); up = u[:, g] == 0
        if g == 6: up = up != mv
        ca[:, g] = np.where(up, large, small); cc[:, g] = np.where(up, small, large)
    return pack(x, lay(b, fl, nu, ca, cc), b, fl, nu, z + 255 * u, z + 255 * (1 - u), th)
def setup_inputs_ends(rng):
    o = 1 + np.argsort(rng.random((N, 8, NB - 2)), axis=-1); k = 1 + np.argsort(rng.random((N, 8, NB - 2)), axis=-1)
    z = np.zeros((N, 8, 1), np.int64); fl = np.concatenate([z, o[..., :P - 2], z + NB - 1], axis=2); nu = np.concatenate([z, k[..., :P - 2], z + NB - 1], axis=2)
    b = np.zeros((N, 8, NB), np.int64); np.put_along_axis(b, fl, k[..., P - 2:], 2); np.put_along_axis(b, o[..., P - 2:], nu, 2)
    rk = 1 + np.argsort(rng.random((N, 8, W - 2)), axis=-1); n = 2 * W // 5; low = rk[:, :, None, :n]; high = rk[:, :, None, n:2 * n]
    x = rng.integers(0, 2, (N, 8, 16, W), dtype=np.int16) * np.int16(255)
    np.put_along_axis(x, low, 0, 3); np.put_along_axis(x, high, 255, 3)
    e = rng.integers(0, 2, (N, 8)); e[N - 1, 7] = 0
    x[..., 0] = 255 * e[:, :, None]; x[..., W - 1] = 255 * (1 - e)[:, :, None]
    eh = np.where(e == 1, 0, W - 1)[:, :, None, None]; el = W - 1 - eh; sh = (N, 8, 16, P)
    ch = np.where(rng.random(sh) < 0.75, eh, np.take_along_axis(high, rng.integers(0, n, sh), 3))
    cl = np.where(rng.random(sh) < 0.75, el, np.take_along_axis(low, rng.integers(0, n, sh), 3))
    u = rng.choice(np.array([0, 0, 1, 1, 2]), (N, 8, 1, P)); u[0] = rng.integers(0, 2, (8, 1, P)); u[N - 1] = rng.integers(0, 2, (8, 1, P)); u[N - 1, 7, 0, P - 1] = 0
    pf = np.where(u == 0, 0, np.where(u == 1, 255, 255 * rng.integers(0, 2, sh))); pn = np.where(u == 0, 255, np.where(u == 1, 0, 255 * rng.integers(0, 2, sh)))
    th = 8159 * rng.integers(0, 2, (N, 8, 16)); th[:, 0, 0] = 0; th[:, 7, 15] = 8159
    w = rng.choice(np.array([0.0, 0.3, 0.6, 0.8, 1.0]), (N, 8, 1, P)); w[0] = 0.0; w[N - 1] = 1.0
    up = (rng.random(sh) < w) == (u == 0); ca = np.where(up, ch, cl); cc = np.where(up, cl, ch)
    tie = rng.random(sh) < 0.1; tie[0] = False; tie[N - 1] = False
    return pack(x, lay(b, fl, nu, ca, np.where(tie, ca, cc)), b, fl, nu, pf, pn, th)
def setup_inputs_fresh(rng):
    b, fl, nu = sites(rng); x, c, pf, pn, th = some(rng); sh = (N, 8, 16, NB)
    sm = np.add.reduce(pf, axis=2); i = rng.integers(0, P, sh); r = np.arange(N)[:, None, None, None]; g = np.arange(8)[None, :, None, None]
    q = (r + ST * rng.integers(0, RO, sh)) % N
    c = np.where(rng.random(sh) < 0.9, Q * i + ((sm[q, g, i] + rng.integers(3, 11, sh)) & (Q - 1)), c)
    return pack(x, c, b, fl, nu, pf, pn, th)
def setup_inputs_spread(rng):
    b, fl, nu = sites(rng)
    x = np.minimum(np.exp2(8.01 * rng.random((N, 8, 1, W), dtype=np.float32)) * rng.random((N, 8, 16, W), dtype=np.float32), 255).astype(np.int16)
    pf = np.minimum(np.exp2(2 + 6.01 * rng.random((N, 8, 1, P))) * rng.random((N, 8, 16, P)), 255).astype(np.int64)
    pn = np.minimum(np.exp2(2 + 6.01 * rng.random((N, 8, 1, P))) * rng.random((N, 8, 16, P)), 255).astype(np.int64)
    c = np.minimum((W * rng.random((N, 8, 16, NB)) ** 3).astype(np.int64), W - 1); c = np.where(rng.random((N, 8, 1, NB)) < 0.5, c, W - 1 - c)
    kind = rng.choice(np.array([0.25, 0.25, 0.5, 1.0]), (N, 8, 1))
    th = np.minimum(np.exp2(13 * kind * rng.random((N, 8, 16))).astype(np.int64) - 1, 8159)
    return pack(x, c, b, fl, nu, pf, pn, th)
def check_inputs(d):
    bad = []
    for k, lo, hi in (("xf", 0, 255), ("cb", 0, W - 1), ("bs", 0, NB - 1), ("fs", 0, NB - 1), ("nb", 0, NB - 1), ("pf", 0, 255), ("pn", 0, 255), ("th", 0, 8159)):
        v = np.asarray(d[k]).astype(np.float32)
        if not (np.all(v >= lo) and np.all(v <= hi)): bad.append("range of " + k)
        elif np.any(v != np.floor(v)): bad.append("whole numbers of " + k)
    b, fl, nu = [np.stack([gentries(np.clip(np.asarray(v), 0, NB - 1).astype(np.int64)) for v in d[k]]) for k in ("bs", "fs", "nb")]
    if np.any(np.sort(b, axis=-1) != np.arange(NB)): bad.append("bs: a permutation of the boxes in every group")
    if np.any(np.sort(np.concatenate([np.take_along_axis(b, fl, -1), nu], axis=2), axis=-1) != np.arange(NB)): bad.append("fs, nb: the flyers' boxes and the nurses' boxes are all boxes, each once")
    return bad
def reference(xf, cb, bs, fs, nb, pf, pn, th):
    x = xf.astype(np.float32).astype(np.int32).reshape(N, 8, 16, W); c = cb.astype(np.int64).reshape(N, 8, 16, NB)
    b, fl, nu = [np.stack([gentries(v) for v in k]).astype(np.int64) for k in (bs, fs, nb)]
    rf = pf.astype(np.float32).astype(np.int32).reshape(N, 8, 16, P); rn = pn.astype(np.float32).astype(np.int32).reshape(N, 8, 16, P); lim = th.astype(np.int64).reshape(N, 8, 16, 1)
    for t in range(RO):
        for r in range(N):
            q = (r + ST * t) % N
            box = np.take_along_axis(b[r], fl[r], 1); nur = nu[r].copy()
            ca = np.take_along_axis(c[r], box[:, None, :], 2); ch = np.take_along_axis(c[r], nur[:, None, :], 2)
            xa = np.take_along_axis(x[q], ca.reshape(8, 1, 16 * P), 2).reshape(8, 16, 16, P)
            xh = np.take_along_axis(x[q], ch.reshape(8, 1, 16 * P), 2).reshape(8, 16, 16, P)
            u = rf[q][:, :, None, :]; v = rn[q][:, :, None, :]
            score = np.add.reduce(np.abs(xa - u) + np.abs(xh - v) - np.abs(xh - u) - np.abs(xa - v), axis=1)
            sw = score > lim[q]; s = np.add.reduce(sw.astype(np.int64), axis=1)
            np.put_along_axis(c[r], box[:, None, :], np.where(sw, ch, ca), 2); np.put_along_axis(c[r], nur[:, None, :], np.where(sw, ca, ch), 2)
            flag = np.zeros((8, NB), bool); np.put_along_axis(flag, fl[r], s >= HI, 1)
            inv = np.argsort(b[r], axis=1); turn = s <= LO
            fl[r] = np.where(turn, np.take_along_axis(inv, nur, 1), fl[r]); nu[r] = np.where(turn, box, nur)
            total = np.add.reduce(s, axis=1)[:, None]
            if not OWN: total = np.zeros((8, 1), np.int64) + np.add.reduce(total, axis=None)
            mate = np.arange(NB)[None, :] ^ ((total & (NB - 1)) | 1)
            both = flag & np.take_along_axis(flag, mate, 1)
            b[r] = np.where(both, np.take_along_axis(b[r], mate, 1), b[r])
            col = Q * np.arange(P)[None, :] + ((np.add.reduce(rf[q].astype(np.int64), axis=1) + s) & (Q - 1))
            np.put_along_axis(x[q], col[:, None, :], rf[q], 2)
    who = [(q - ST * (RO - 1)) % N for q in range(N)]
    return {"yc": c[who].reshape(N, 128, NB).astype(np.float32), "yb": np.stack([gtable(b[r]) for r in who]).astype(np.float32),
            "yf": np.stack([gtable(fl[r]) for r in who]).astype(np.float32), "yn": np.stack([gtable(nu[r]) for r in who]).astype(np.float32)}

@@ -1,0 +1,566 @@
+from concourse.mybir import AluOpType as A, AxisListType, ActivationFunctionType as AF
+
+NS = ((), (5, 6, 7))
+NSET = (5, 6, 7)
+NXG, NT = 8, 2
+LG = 6
+LP = 3
+WCOL = 544
+FL, BF, I32, U16 = "float32", "bfloat16", "int32", "uint16"
+
+
+def _scratch():
+    s = {}
+
+    def sb(names, cols, dt):
+        for n in names.split():
+            s[n] = ("sbuf", [128, cols], dt)
+    sb("xfs", 8192, BF)
+    sb("F16 N16", 4096, BF)
+    sb("FMN NNEG", 512 * len(NSET), BF)
+    sb("pfs pns FLB MROW IDX1 XN", 256, BF)
+    sb("cbs", 512, I32)
+    sb("CBF CS YC", 512, FL)
+    sb("bss", 32, I32)
+    sb("fss nbs OI1 OI2 OI3 BASE LI", 16, I32)
+    sb("ths TI PI PM UI UB", 2, I32)
+    sb("BITS", 16, I32)
+    sb("thl thh PMF RTOT CF AB C128", 2, FL)
+    sb("ONES", 128, BF)
+    sb("IDENT G16", 128, BF)
+    sb("SELP", 2048, BF)
+    sb("SWT THH THL", 128, BF)
+    sb("GN8", 8, BF)
+    sb("XG", 512 * NXG, BF)
+    sb("TF TN", 2048 * NT, BF)
+    sb("OH OA", 256, U16)
+    sb("CAf CHf DD", 256, FL)
+    sb("SW", 256, BF)
+    sb("WI1 WI2 WI3 WI4 WO0 WO1 WO2 WO3 WO4", WCOL, FL)
+    sb("MI0 MI1 MI2 MI3 MI4 MO0 MO1 MO2 MO3 MO4", 64, FL)
+    sb("HI1 HI2", 32, FL)
+    sb("bsU XLU XLS YL GU", 32, U16)
+    sb("fsU nbU FU ETAU ALU OFFU E4U", 16, U16)
+    sb("DFG TRN XX TD FL16 ABS Z1 Z2 Z3 LIF LI1 AB0 ELS", 16, FL)
+    sb("U", 1536, BF)
+    sb("IOTC BROW BROW4", 512, BF)
+    sb("XB0 XB1", WCOL, BF)
+    sb("GROW", 256, BF)
+    sb("RS RC", 32, BF)
+    sb("LB", 128, BF)
+    sb("LTB RTB", 16, BF)
+    sb("PAB", 48, FL)
+    sb("BL B1 B2 B3 B4 YB", 32, FL)
+    for n in ["PX0", "PX1", "PX2", "PX3", "PSC0", "PSC1", "PL", "PM2"]:
+        s[n] = ("psum", [128, 512], FL)
+    return s
+
+
+SCRATCH = _scratch()
+LOADS = ["pf", "pn", "fs", "bs", "nb", "th", "cb", "xa", "xb"]
+SEMAPHORES = (["qV", "qS", "qP", "qG", "loc"] + ["d_" + n for n in LOADS] + ["o_yc", "o_yb", "o_yf", "o_yn"]
+              + ["a%d_%d" % (k, t) for k in range(5) for t in range(1, 5)] + ["ah1", "ah2"])
+
+
+def rank_program(g, core, T, topo):
+    rank = T.rank_of(core)
+    if rank is None:
+        return
+    N = len(T.cores)
+    Q = {"V": g.vector, "S": g.scalar, "P": g.tensor, "G": g, "D": g.sync}
+    cnt = {"V": 0, "S": 0, "P": 0, "G": 0}
+    seen = {q: {} for q in Q}
+    snap = {}
+    wr, wp, rd = {}, {}, {}
+
+    def need(q, R, W):
+        toks = []
+        for k in R:
+            if k in wr:
+                toks.append(wr[k])
+            if k[0] == "P":
+                toks += [t for qq, t in rd.get(k, {}).items() if qq != q]
+        for k in W:
+            w = wr if k[0] != "+" else wp
+            k = k.lstrip("+")
+            if k in w and (q != "P" or w[k][0] != "qP"):
+                toks.append(w[k])
+            toks += [t for qq, t in rd.get(k, {}).items() if q != "P" or qq != q]
+        best = {}
+        for s, v in toks:
+            if v > seen[q].get(s, 0):
+                best[s] = max(best.get(s, 0), v)
+        for s in sorted(best, key=lambda s: -best[s]):
+            v = best[s]
+            if v <= seen[q].get(s, 0):
+                continue
+            Q[q].wait_ge(T.sem[s], v)
+            for s2, v2 in snap.get((s, v), {}).items():
+                seen[q][s2] = max(seen[q].get(s2, 0), v2)
+            seen[q][s] = max(seen[q].get(s, 0), v)
+
+    def done(q, R, W, tok):
+        snap[tok] = dict(seen[q])
+        for k in R:
+            rd.setdefault(k, {})[q] = tok
+        for k in W:
+            wr[k.lstrip("+")] = tok
+            if k[0] != "+":
+                wp[k] = tok
+                rd[k] = {}
+
+    def op(q, fn, R, W):
+        R, W = R.split(), W.split()
+        need(q, R, W)
+        fn(Q[q]).then_inc(T.sem["q" + q], 1)
+        cnt[q] += 1
+        done(q, R, W, ("q" + q, cnt[q]))
+
+    def dma(q, out, in_, R, W, sem):
+        R, W = R.split(), W.split()
+        need(q, R, W)
+        Q[q].dma_start(out, in_).then_inc(T.sem[sem], 16)
+        done(q, R, W, (sem, 16))
+
+    nloc = [0]
+
+    def send(dst, out, in_, R, sem):
+        need("G", R.split(), [])
+        m = topo.mask(core, dst)
+        rid, pid, _s = topo.addr(dst)
+        g.remote_dma(out, in_, T.sem[sem], T.sem.loc, pid, rid, m)
+        nloc[0] += len(topo.engines(core, dst))
+
+    for t in range(1, 5):
+        src = T.cores[(rank - 1) % N]
+        ne = len(topo.engines(src, core))
+        wr["WI%da" % t] = ("a0_%d" % t, ne)
+        wr["WI%db" % t] = ("a1_%d" % t, ne)
+        wr["WI%de0" % t] = ("a3_%d" % t, ne)
+        wr["WI%de1" % t] = ("a4_%d" % t, ne)
+        wr["MI%d" % t] = ("a2_%d" % t, ne)
+    wr["HI1"] = ("ah1", len(topo.engines(T.cores[(rank + 1) % N], core)))
+    wr["HI2"] = ("ah2", len(topo.engines(T.cores[(rank + 2) % N], core)))
+
+    def tt(o, a, b, o_, R, W):
+        op("V", lambda e: e.tensor_tensor(o, a, b, o_), R, W)
+
+    def ts(o, a, s1, s2, o0, o1, R, W):
+        if o1 is None:
+            op("V", lambda e: e.tensor_scalar(o, a, s1, None, o0), R, W)
+        else:
+            op("V", lambda e: e.tensor_scalar(o, a, s1, s2, o0, o1), R, W)
+
+    def cp(o, a, R, W):
+        op("V", lambda e: e.tensor_copy(o, a), R, W)
+
+    def ms(o, c, W):
+        op("V", lambda e: e.memset(o, c), "", W)
+
+    def act(o, a, R, W, f=AF.Copy, **kw):
+        op("S", lambda e: e.activation(o, a, f, **kw), R, W)
+
+    def mm(o, l, r, st, sp, R, W):
+        op("P", lambda e: e.matmul(o, l, r, st, sp), R, W)
+
+    def sel(k):
+        return T.SELP[:, 128 * k:128 * k + 128]
+
+    def conv(out, row, a, n, R, W):
+        for l in range(16):
+            mm(out, sel(l), row[:, a + l:a + 16 * (n - 1) + l + 1:16], l == 0, l == 15, R + " SELP", W)
+
+    dma("D", T.nbs[:], T.nb[:], "", "nbs", "d_nb")
+    dma("S", T.cbs[:], T.cb[:], "", "cbs", "d_cb")
+    dma("D", T.bss[:], T.bs[:], "", "bss", "d_bs")
+    dma("S", T.pns[:], T.pn[:], "", "pns", "d_pn")
+    dma("D", T.fss[:], T.fs[:], "", "fss", "d_fs")
+    dma("D", T.pfs[:], T.pf[:], "", "pfs", "d_pf")
+    dma("D", T.ths[:, 0:1], T.th[:], "", "ths", "d_th")
+    dma("S", T.xfs[:, 0:4096], T.xf[:, 0:4096], "", "xfs", "d_xa")
+    dma("D", T.xfs[:, 4096:8192], T.xf[:, 4096:8192], "", "xfsb", "d_xb")
+
+    def gop(fn, R, W):
+        op("G", fn, R, W)
+    ms(T.ONES[:], 1.0, "ONES")
+    ms(T.SELP[:], 0.0, "SELP")
+    gop(lambda e: e.iota(T.IOTC[:], [[1, 512]], -256, 0, allow_small_or_imprecise_dtypes=True), "", "IOTC")
+    gop(lambda e: e.affine_select(T.SWT[:], T.ONES[:], [[-16, 8], [0, 16]], A.is_ge, 0.0, 0, 1), "ONES", "SWT")
+    gop(lambda e: e.affine_select(T.G16[:], T.SWT[:], [[16, 8], [0, 16]], A.is_ge, 0.0, 15, -1), "SWT", "G16")
+    gop(lambda e: e.affine_select(T.IDENT[:], T.ONES[:], [[-1, 128]], A.is_equal, 0.0, 0, 1), "ONES", "IDENT")
+    gop(lambda e: e.iota(T.PI[:, 0:1], [[1, 1]], 0, 1), "", "PI")
+    gop(lambda e: e.iota(T.LI[:], [[16, 16]], 0, 0), "", "LI")
+    gop(lambda e: e.iota(T.IDX1[:], [[1, 256]], 1, 0, allow_small_or_imprecise_dtypes=True), "", "IDX1")
+    for t in range(5):
+        for c in (8, 536):
+            gop(lambda e: e.iota(T["WO%d" % t][:, c:c + 8], [[0, 8]], 0, 0, allow_small_or_imprecise_dtypes=True), "", "WO%dp" % t)
+    cp(T.fsU[:], T.fss[:], "fss", "fsU")
+    cp(T.bsU[:], T.bss[:], "bss", "bsU")
+    cp(T.nbU[:], T.nbs[:], "nbs", "nbU")
+    cp(T.CBF[:], T.cbs[:], "cbs", "CBF")
+    cp(T.OH[:], T.CBF[:].indirect(T.nbU[:]), "CBF nbU", "OHa OHb")
+    act(T.CS[:], T.CBF[:].indirect(T.bsU[:]), "CBF bsU", "CS")
+    for k in range(16):
+        cp(T.F16[:, k::16], T.pfs[:], "pfs", "+F16")
+        act(T.N16[:, k::16], T.pns[:], "pns", "+N16")
+    cp(T.OA[:], T.CS[:].indirect(T.fsU[:]), "CS fsU", "OA")
+    for k in range(16):
+        cp(T.SELP[:, 128 * k + k:128 * k + 128:16], T.G16[:, k::16], "G16", "+SELP")
+    ts(T.GN8[:], T.G16[:, ::16], -1.0, None, A.mult, None, "G16", "GN8")
+    for n, c in enumerate(NSET):
+        d, s = slice(512 * n, 512 * n + 512), slice(512 * c, 512 * c + 512)
+        ts(T.NNEG[:, d], T.N16[:, s], -1.0, None, A.mult, None, "N16", "+NNEG")
+        tt(T.FMN[:, d], T.F16[:, s], T.N16[:, s], A.subtract, "F16 N16", "+FMN")
+    for n, (bits, f, c) in enumerate(((4032, "thh", "THH"), (63, "thl", "THL"))):
+        op("V", lambda e: e.tensor_scalar(T.TI[:, n:n + 1], T.ths[:, 0:1], 1, bits, A.arith_shift_right, A.bitwise_and), "ths", "TI%d" % n)
+        cp(T[f][:, 0:1], T.TI[:, n:n + 1], "TI%d" % n, f)
+        ts(T[c][:], T.ONES[:], T[f][:, 0:1], -1.0, A.mult, A.mult, "ONES " + f, c)
+
+    def setup_lists():
+        op("V", lambda e: e.tensor_scalar(T.PM[:, 0:1], T.PI[:, 0:1], 15, None, A.bitwise_and), "PI", "PM")
+        cp(T.PMF[:, 0:1], T.PM[:, 0:1], "PM", "PMF")
+        ts(T.LIF[:], T.LI[:], T.PMF[:, 0:1], None, A.add, None, "LI PMF", "LIF")
+        ts(T.BASE[:], T.LIF[:], 32.0, None, A.mult, None, "LIF", "BASE")
+        ts(T.LI1[:], T.LIF[:], 1.0, None, A.add, None, "LIF", "LI1")
+        ts(T.AB0[:], T.LIF[:], 144.0, None, A.add, None, "LIF", "AB0")
+        conv(T.PL[:, 0:16], T.pfs, 0, 16, "pfs", "PL")
+        cp(T.ELS[:], T.PL[:, 0:16], "PL", "ELS")
+        cp(T.MI0[:, 0:16], T.fss[:], "fss", "MI0")
+        cp(T.BROW4[:].indirect(T.bsU[:]), T.IOTC[:], "IOTC bsU", "BROW4")
+        act(T.GROW[:], T.BROW4[:].indirect(T.nbU[:]), "BROW4 nbU", "GROW")
+        conv(T.PL[:, 16:32], T.GROW, 0, 16, "GROW", "PL")
+        ts(T.MI0[:, 16:32], T.PL[:, 16:32], 0.0625, 256.0, A.mult, A.add, "PL", "MI0")
+
+    def setup_xor():
+        for b in range(4):
+            op("V", lambda e: e.tensor_scalar(T.BITS[:, b:b + 1], T.PM[:, 0:1], b, 1, A.arith_shift_right, A.bitwise_and), "PM", "+BITS")
+        for b in range(5):
+            op("V", lambda e: e.tensor_scalar(T.BITS[:, 4 + b:5 + b], T.PI[:, 0:1], b, 1, A.arith_shift_right, A.bitwise_and), "PI", "+BITS")
+        ms(T.LTB[:], 1.0, "LTB")
+        ms(T.RTB[:], 1.0, "RTB")
+        ts(T.LTB[:, 0:4], T.BITS[:, 0:4], -2.0, 1.0, A.mult, A.add, "BITS", "LTB")
+        ts(T.RTB[:, 4:9], T.BITS[:, 4:9], -2.0, 1.0, A.mult, A.add, "BITS", "RTB")
+        for b in range(9):
+            ms(T.PAB[:, b:b + 1], float(2 ** (8 - b)), "+POW")
+            ms(T.PAB[:, 16 + b:17 + b], 2.0 ** b / 256 if b else 0.0, "+AC")
+            ms(T.PAB[:, 32 + b:33 + b], -2.0 ** (b - 1) if b else 0.5, "+BC")
+        ms(T.C128[:, 0:1], 1.0 / 128, "C128")
+        mm(T.PM2[0:9, 0:128], T.LTB[:, 0:9], T.IDENT[:], True, True, "LTB IDENT", "PM2")
+        mm(T.PM2[0:9, 128:160], T.RTB[0:32, 0:9], T.IDENT[0:32, 0:32], True, True, "RTB IDENT", "PM2")
+        mm(T.PM2[0:9, 160:161], T.PAB[:, 16:25], T.C128[:, 0:1], True, True, "AC C128", "PM2")
+        mm(T.PM2[0:9, 161:162], T.PAB[:, 32:41], T.C128[:, 0:1], True, True, "BC C128", "PM2")
+        cp(T.LB[0:9, :], T.PM2[0:9, 0:128], "PM2", "LB")
+        cp(T.RC[0:9, :], T.PM2[0:9, 128:160], "PM2", "RC")
+        cp(T.AB[0:9, 0:2], T.PM2[0:9, 160:162], "PM2", "AB")
+
+    def setup_boxes():
+        ms(T.XB0[:], 0.0, "XB0")
+        ms(T.XB1[:], 0.0, "XB1")
+        act(T.BROW[:], T.IOTC[:].indirect(T.bsU[:]), "IOTC bsU", "BROW")
+        act(T.XB0[:, 144:400], T.BROW[:].indirect(T.fsU[:]), "BROW fsU", "XB0")
+        act(T.XB0[:, 16:144], T.IOTC[:].indirect(T.nbU[:, 0:8]), "IOTC nbU", "XB0")
+        act(T.XB0[:, 400:528], T.IOTC[:].indirect(T.nbU[:, 8:16]), "IOTC nbU", "XB0")
+
+    def xg(j):
+        return T.XG[:, 512 * (j % NXG):512 * (j % NXG) + 512]
+
+    def gather(j):
+        off = T.OH if j < 8 else T.OA
+        key = ("OHa" if j < 4 else "OHb") if j < 8 else "OA"
+        c = j % 8
+        act(xg(j), T.xfs[:].indirect(off[:, 32 * c:32 * c + 32]), "xfs xfsb " + key, "XG%d" % (j % NXG))
+
+    def ident(j):
+        c, b = j % 8, "PX%d" % (j % 4)
+        x = "XG%d" % (j % NXG)
+        if c in NS[j // 8]:
+            n = NSET.index(c)
+            mm(T[b][:], T.IDENT[:], xg(j), True, False, "IDENT " + x, b)
+            mm(T[b][:], T.IDENT[:], T.NNEG[:, 512 * n:512 * n + 512], False, True, "IDENT NNEG", b)
+        else:
+            mm(T[b][:], T.IDENT[:], xg(j), True, True, "IDENT " + x, b)
+
+    def term_f(j):
+        c, b, n = j % 8, "PX%d" % (j % 4), (j // 4) % NT
+        o = T.TF[:, 512 * (j % 8):512 * (j % 8) + 512]
+        if c in NS[j // 8]:
+            tab, key, a = T.FMN, "FMN", NSET.index(c)
+        else:
+            tab, key, a = T.F16, "F16", c
+        tt(o, T[b][:], tab[:, 512 * a:512 * a + 512], A.max, b + " " + key, "TF%d_%d" % (n, j % 4))
+
+    def term_n(j):
+        c, b, n = j % 8, "PX%d" % (j % 4), (j // 4) % NT
+        o = T.TN[:, 512 * (j % 8):512 * (j % 8) + 512]
+        if c in NS[j // 8]:
+            act(o, T[b][:], b, "TN%d_%d" % (n, j % 4), f=AF.Relu)
+        else:
+            tt(o, T[b][:], T.N16[:, 512 * c:512 * c + 512], A.max, b + " N16", "TN%d_%d" % (n, j % 4))
+
+    def lanes(blk, which):
+        a, h = blk >= 2, blk % 2
+        nm = "%s%d" % (("TF", "TN")[which], blk % NT)
+        P = "PSC%d" % h
+        if not a and which == 0:
+            mm(T[P][:, 0:128], T.THH[:], T.IDENT[:], True, False, "THH IDENT", P)
+            mm(T[P][:, 0:128], T.THL[:], T.IDENT[:], False, False, "THL IDENT", P)
+        tab, key = (T.G16[:, ::16], "G16") if a == (which == 0) else (T.GN8[:], "GN8")
+        for k in range(16):
+            o = 2048 * (blk % NT)
+            mm(T[P][:, k:128:16], T[nm[0:2]][:, o + k:o + 2048:16], tab, False, a and which == 1 and k == 15,
+               "%s_0 %s_1 %s_2 %s_3 %s" % (nm, nm, nm, nm, key), P)
+
+    def half_cmp(h):
+        ts(T.SWT[:], T["PSC%d" % h][:, 0:128], 0.0, None, A.is_gt, None, "PSC%d" % h, "SWT")
+        mm(T.PM2[:, 256:384], T.SWT[:], T.IDENT[:], True, True, "SWT IDENT", "PM2")
+
+    def half_sum(h):
+        cp(T.SW[:, 128 * h:128 * h + 128], T.PM2[:, 256:384], "PM2", "SW%d" % h)
+        conv(T.PL[:, 8 * h:8 * h + 8], T.SW, 128 * h, 8, "SW%d" % h, "PL")
+
+    def half_rows(t, h):
+        s = slice(128 * h, 128 * h + 128)
+        wo, key = T["WO%d" % t], "WO%d%s" % (t, "ab"[h])
+        p = T.PM2[:, 256:384]
+        tt(p, p, T.DD[:, s], A.mult, "DD%d PM2" % h, "PM2")
+        a = slice(144 + 128 * h, 272 + 128 * h)
+        hh = slice(16 + 384 * h, 144 + 384 * h)
+        tt(wo[:, a], p, T.CAf[:, s], A.add, "PM2 CAf", "+" + key)
+        tt(wo[:, hh], T.CHf[:, s], p, A.subtract, "PM2 CHf%d" % h, "+" + key)
+        if t < 4:
+            w = slice(16 + 256 * h, 272 + 256 * h)
+            send(T.cores[(rank + 1) % N], T["WI%d" % (t + 1)][:, w], wo[:, w], key, "a%d_%d" % (h, t + 1))
+
+    def half_off(h):
+        s = slice(8 * h, 8 * h + 8)
+        tt(T.OI1[:, s], T.PL[:, s], T.ELS[:, s], A.add, "PL ELS", "OI1")
+        op("V", lambda e: e.tensor_scalar(T.OI2[:, s], T.OI1[:, s], 31, None, A.bitwise_and), "OI1", "OI2")
+        tt(T.OI3[:, s], T.OI2[:, s], T.BASE[:, s], A.add, "OI2 BASE", "OI3")
+        cp(T.OFFU[:, s], T.OI3[:, s], "OI3", "OFFU%d" % h)
+
+    def half_put(h):
+        s, r = slice(8 * h, 8 * h + 8), slice(128 * h, 128 * h + 128)
+        cp(T.xfs[:].indirect(T.OFFU[:, s]), T.pfs[:, r], "pfs OFFU%d" % h, "xfs xfsb")
+
+    def half_eta(t, h):
+        s = slice(8 * h, 8 * h + 8)
+        wo, key = T["WO%d" % t], "WO%d%s" % (t, "ab"[h])
+        e = slice(528 * h, 528 * h + 16)
+        ts(T.TD[:, s], T.PL[:, s], 4.5, (-128.0, 128.0)[h], A.is_lt, A.mult, "PL", "TD%d" % h)
+        tt(wo[:, 528 * h:528 * h + 8], T.LIF[:, s], T.TD[:, s], A.subtract, "LIF TD%d" % h, "WO%de%d" % (t, h))
+        if t < 4:
+            send(T.cores[(rank + 1) % N], T["WI%d" % (t + 1)][:, e], wo[:, e], "WO%de%d WO%dp" % (t, h, t), "a%d_%d" % (3 + h, t + 1))
+            act(T["MO%d" % t][:, 32 + 24 * h:40 + 24 * h], wo[:, 528 * h:528 * h + 8], "WO%de%d" % (t, h), "MO%de%d" % (t, h),
+                f=AF.Identity, bias=(16.0, 272.0)[h])
+
+    def win(t, h):
+        return T["WI%d" % t][:, 16 + 256 * h:272 + 256 * h]
+
+    def take_h(t, h):
+        s = slice(8 * h, 8 * h + 8)
+        cp(T.ETAU[:, s], T["WI%d" % t][:, 528 * h:528 * h + 8], "WI%de%d" % (t, h), "ETAU%d" % h)
+        cp(T.OH[:, 128 * h:128 * h + 128], win(t, h).indirect(T.ETAU[:, s]), "WI%d%s ETAU%d" % (t, "ab"[h], h), "OH" + "ab"[h])
+
+    def all_in(t):
+        return "WI%da WI%db WI%de0 WI%de1 " % (t, t, t, t)
+
+    def take_a(t):
+        cp(T.ALU[:], T["MI%d" % t][:, 40:56], "MI%d" % t, "ALU")
+        cp(T.OA[:], T["WI%d" % t][:].indirect(T.ALU[:]), all_in(t) + "ALU", "OA")
+
+    def floats(t, part):
+        if t == 0:
+            if part < 2:
+                h = part
+                act(T.CHf[:, 128 * h:128 * h + 128], T.CBF[:].indirect(T.nbU[:, 8 * h:8 * h + 8]), "CBF nbU", "CHf%d" % h)
+            else:
+                act(T.CAf[:], T.CS[:].indirect(T.fsU[:]), "CS fsU", "CAf")
+        elif part < 2:
+            h = part
+            act(T.CHf[:, 128 * h:128 * h + 128], win(t, h).indirect(T.ETAU[:, 8 * h:8 * h + 8]), "WI%d%s ETAU%d" % (t, "ab"[h], h), "CHf%d" % h)
+        else:
+            act(T.CAf[:], T["WI%d" % t][:].indirect(T.ALU[:]), all_in(t) + "ALU", "CAf")
+
+    def diff(h):
+        s = slice(128 * h, 128 * h + 128)
+        tt(T.DD[:, s], T.CHf[:, s], T.CAf[:, s], A.subtract, "CAf CHf%d" % h, "DD%d" % h)
+
+    def sites_in(t):
+        m = "MI%d" % t
+        cp(T.FU[:], T[m][:, 0:16], m, "FU")
+        tt(T.DFG[:], T[m][:, 16:32], T[m][:, 0:16], A.subtract, m, "DFG")
+
+    def chain(t):
+        op("V", lambda e: e.tensor_reduce(T.RTOT[:, 0:1], T.PL[:, 0:16], AxisListType.X, A.add), "PL", "RTOT")
+        mm(T.PM2[0:9, 384:385], T.PAB[:, 0:9], T.RTOT[:, 0:1], True, True, "POW RTOT", "PM2")
+        ts(T.TRN[:], T.PL[:, 0:16], 4.5, None, A.is_lt, None, "PL", "TRN")
+        cp(T.UI[0:9, 0:1], T.PM2[0:9, 384:385], "PM2", "UI")
+        op("V", lambda e: e.tensor_scalar(T.UB[0:9, 0:1], T.UI[0:9, 0:1], 256, None, A.bitwise_and), "UI", "UB")
+        if t < 4:
+            ts(T.FL16[:], T.PL[:, 0:16], 8.5, 0.0625, A.is_gt, A.mult, "PL", "FL16")
+        ts(T.CF[0:9, 0:1], T.UB[0:9, 0:1], T.AB[0:9, 0:1], T.AB[0:9, 1:2], A.mult, A.add, "UB AB", "CF")
+        tt(T.XX[:], T.TRN[:], T.DFG[:], A.mult, "TRN DFG", "XX")
+        ts(T.RS[0:9, :], T.RC[0:9, :], T.CF[0:9, 0:1], None, A.mult, None, "RC CF", "RS")
+        mm(T.PM2[:, 400:432], T.LB[0:9, :], T.RS[0:9, :], True, True, "LB RS", "PM2")
+        mm(T.PM2[:, 0:256], T.G16[:], T.SW[:], True, True, "G16 SW0 SW1", "PM2")
+        if t < 4:
+            take_h(t + 1, 0)
+        m, mo = "MI%d" % t, "MO%d" % t
+        tt(T[mo][:, 0:16], T[m][:, 0:16], T.XX[:], A.add, m + " XX", mo)
+        ts(T.XLU[:], T.PM2[:, 400:432], 255.5, None, A.add, None, "PM2", "XLU")
+        ts(T.FLB[:], T.PM2[:, 0:256], 8.5, None, A.is_gt, None, "PM2", "FLB")
+        tt(T.U[:, 0:512].indirect(T.FU[:]), T.FLB[:], T.IDX1[:], A.mult, "FLB IDX1 FU", "U0")
+        if t < 4:
+            tt(T[mo][:, 16:32], T[m][:, 16:32], T.XX[:], A.subtract, m + " XX", mo)
+            tt(T.ABS[:], T.AB0[:], T.TD[:], A.add, "AB0 TD0 TD1", "ABS")
+
+    def partner(t):
+        act(T.U[:, 512:1024], T.U[:, 0:512].indirect(T.XLU[:]), "U0 XLU", "U1")
+        act(T.MROW[:], T.U[:, 512:1024].indirect(T.FU[:]), "U1 FU", "MROW")
+        conv(T.PL[:, 32:48], T.MROW, 0, 16, "MROW", "PL")
+
+    def alpha(t):
+        mo = "MO%d" % t
+        tt(T.Z1[:], T.PL[:, 32:48], T.FL16[:], A.mult, "PL FL16", "Z1")
+        ts(T.Z2[:], T.Z1[:], 256.0, None, A.mult, None, "Z1", "Z2")
+        tt(T.Z1[:], T.Z1[:], T.ABS[:], A.add, "Z1 ABS", "Z1")
+        tt(T.Z3[:], T.Z2[:], T.LI1[:], A.min, "Z2 LI1", "Z3")
+        tt(T[mo][:, 40:56], T.Z1[:], T.Z3[:], A.subtract, "Z1 Z3", mo)
+        mo += " %se0 %se1" % (mo, mo)
+        send(T.cores[(rank + 1) % N], T["MI%d" % (t + 1)][:], T["MO%d" % t][:], mo, "a2_%d" % (t + 1))
+        if t in (1, 2):
+            send(T.cores[(rank - t) % N], T["HI%d" % t][:], T["MO%d" % t][:, 32:64], mo, "ah%d" % t)
+
+    def boxes(n, lists, key):
+        a, b = "XB%d" % (n % 2), "XB%d" % (1 - n % 2)
+        cp(T.XLS[:], lists, key, "XLS")
+        act(T[b][:, 16:528], T[a][:].indirect(T.XLS[:]), a + " XLS", b)
+
+    def box_lists():
+        conv(T.PL[:, 64:96], T.XB0, 16, 32, "XB0", "PL")
+        ts(T.YL[:], T.PL[:, 64:96], 0.0625, 256.0, A.mult, A.add, "PL", "YL")
+        cp(T.GU[:, 0:8], T.MI4[:, 16:24], "MI4", "GU")
+        cp(T.GU[:, 8:24], T.MI4[:, 0:16], "MI4", "+GU")
+        cp(T.GU[:, 24:32], T.MI4[:, 24:32], "MI4", "+GU")
+
+    def brow4():
+        cp(T.BROW4[:].indirect(T.GU[:]), T.XB0[:, 16:528], "XB0 GU", "BROW4")
+        conv(T.PL[:, 128:160], T.BROW4, 0, 32, "BROW4", "PL")
+        ts(T.BL[:], T.PL[:, 128:160], 0.0625, 256.0, A.mult, A.add, "PL", "BL")
+
+    def put_yc(h):
+        k = "WO4" + "ab"[h]
+        cp(T.YC[:].indirect(T.YL[:, 16 * h:16 * h + 16]), T.WO4[:, 16 + 256 * h:272 + 256 * h], k + " YL", "YC")
+
+    def main(t):
+        st = {"g": 0, "p": 0}
+
+        def ahead(j):
+            lim = 4 if not st.get("oh1") else (8 if not st.get("oa") else 16)
+            while st["g"] < min(lim, j + LG if j else 3):
+                gather(st["g"])
+                st["g"] += 1
+            while st["p"] < min(st["g"], j + LP + 1, 16):
+                ident(st["p"])
+                st["p"] += 1
+        if t == 0:
+            st["oh1"] = st["oa"] = True
+        for j in range(16):
+            ahead(j)
+            if j == 1 and t:
+                partner(t - 1)
+            if j == 3 and t:
+                alpha(t - 1)
+            if j == 2 and t:
+                take_h(t, 1)
+                st["oh1"] = True
+                ahead(j)
+            if j == 2 and t == 0:
+                setup_lists()
+            if j == 3 and t == 0:
+                setup_xor()
+            if j == 4 and t == 0:
+                setup_boxes()
+            if j == 5:
+                floats(t, 0)
+                floats(t, 1)
+            if j == 6 and t:
+                take_a(t)
+                st["oa"] = True
+                ahead(j)
+            if j == 9:
+                floats(t, 2)
+                sites_in(t)
+            if j == 13:
+                diff(0)
+                diff(1)
+            if t == 1 and j == 10:
+                boxes(0, T.MO0[:, 32:64], "MO0")
+            if t == 3 and j == 9:
+                boxes(1, T.HI1[:], "HI1")
+            if t == 3 and j == 11:
+                boxes(2, T.HI2[:], "HI2")
+            if t == 4 and j == 8:
+                boxes(3, T.MI4[:, 32:64], "MI4")
+            if t == 4 and j == 11:
+                box_lists()
+            if t == 4 and j == 12:
+                brow4()
+            if j == 14:
+                half_cmp(0)
+            term_f(j)
+            if j == 14:
+                half_sum(0)
+                half_rows(t, 0)
+            term_n(j)
+            if j < 12:
+                if j % 4 == 3:
+                    lanes(j // 4, 0)
+                    lanes(j // 4, 1)
+        lanes(3, 0)
+        lanes(3, 1)
+        act(T.U[:, 0:512], T.IOTC[:], "IOTC", "U0", scale=0.0)
+        half_eta(t, 0)
+        if t < 4:
+            half_off(0)
+            half_put(0)
+        else:
+            put_yc(0)
+        half_cmp(1)
+        half_sum(1)
+        half_rows(t, 1)
+        if t < 4:
+            half_off(1)
+            half_put(1)
+        else:
+            put_yc(1)
+            dma("D", T.yc[:], T.YC[:], "YC", "yc", "o_yc")
+        half_eta(t, 1)
+        chain(t)
+
+    for t in range(5):
+        main(t)
+
+    dma("D", T.yf[:], T.MO4[:, 0:16], "MO4", "yf", "o_yf")
+    act(T.U[:, 512:1024], T.U[:, 0:512].indirect(T.XLU[:]), "U0 XLU", "U1")
+    act(T.U[:, 1024:1536], T.BROW4[:].indirect(T.XLU[:]), "BROW4 XLU", "U2")
+    conv(T.PL[:, 192:288], T.U, 0, 96, "U0 U1 U2", "PL")
+    ts(T.E4U[:, 0:8], T.WO4[:, 0:8], 16.0, None, A.add, None, "WO4e0", "E4U")
+    ts(T.E4U[:, 8:16], T.WO4[:, 528:536], 272.0, None, A.add, None, "WO4e1", "E4U")
+    act(T.XN[:], T.XB0[:].indirect(T.E4U[:]), "XB0 E4U", "XN")
+    ts(T.B1[:], T.PL[:, 192:224], 0.5, None, A.is_gt, None, "PL", "B1")
+    ts(T.B2[:], T.PL[:, 224:256], 0.5, None, A.is_gt, None, "PL", "B2")
+    ts(T.B3[:], T.PL[:, 256:288], 0.0625, 256.0, A.mult, A.add, "PL", "B3")
+    tt(T.B1[:], T.B1[:], T.B2[:], A.mult, "B1 B2", "B1")
+    tt(T.B3[:], T.B3[:], T.BL[:], A.subtract, "B3 BL", "B3")
+    tt(T.B4[:], T.B3[:], T.B1[:], A.mult, "B3 B1", "B4")
+    tt(T.YB[:], T.BL[:], T.B4[:], A.add, "BL B4", "YB")
+    dma("D", T.yb[:], T.YB[:], "YB", "yb", "o_yb")
+    conv(T.PL[:, 320:336], T.XN, 0, 16, "XN", "PL")
+    ts(T.Z3[:], T.PL[:, 320:336], 0.0625, 256.0, A.mult, A.add, "PL", "Z3")
+    dma("D", T.yn[:], T.Z3[:], "Z3", "yn", "o_yn")
+    for q in ("V", "S", "P", "G"):
+        g.wait_ge(T.sem["q" + q], cnt[q])
+    for n in ("yc", "yb", "yf", "yn"):
+        g.wait_ge(T.sem["o_" + n], 16)
+    g.wait_ge(T.sem.loc, nloc[0])

@@ -3,8 +3,9 @@ from concourse.mybir import AluOpType as A, AxisListType, ActivationFunctionType
 NS = ((), (5, 6, 7))
 NSET = (5, 6, 7)
 NXG, NT = 8, 2
-LG = 6
-LP = 3
+LG = 7
+JF, JD, JC, JS = 9, 14, 14, 14
+LP = 2
 WCOL = 544
 FL, BF, I32, U16 = "float32", "bfloat16", "int32", "uint16"
 
@@ -22,10 +23,11 @@ def _scratch():
     sb("cbs", 512, I32)
     sb("CBF CS YC", 512, FL)
     sb("bss", 32, I32)
-    sb("fss nbs OI1 OI2 OI3 BASE LI", 16, I32)
+    sb("fss nbs OI1 OI2 BASE LI", 16, I32)
     sb("ths TI PI PM UI UB", 2, I32)
     sb("BITS", 16, I32)
-    sb("thl thh PMF RTOT CF AB C128", 2, FL)
+    sb("IDF NIDF", 128, FL)
+    sb("NB thh PMF RTOT CF AB C128", 2, FL)
     sb("ONES", 128, BF)
     sb("IDENT G16", 128, BF)
     sb("SELP", 2048, BF)
@@ -34,7 +36,7 @@ def _scratch():
     sb("XG", 512 * NXG, BF)
     sb("TF TN", 2048 * NT, BF)
     sb("OH OA", 256, U16)
-    sb("CAf CHf DD", 256, FL)
+    sb("CAf CHf", 256, FL)
     sb("SW", 256, BF)
     sb("WI1 WI2 WI3 WI4 WO0 WO1 WO2 WO3 WO4", WCOL, FL)
     sb("MI0 MI1 MI2 MI3 MI4 MO0 MO1 MO2 MO3 MO4", 64, FL)
@@ -175,7 +177,7 @@ def rank_program(g, core, T, topo):
     dma("D", T.bss[:], T.bs[:], "", "bss", "d_bs")
     dma("S", T.pns[:], T.pn[:], "", "pns", "d_pn")
     dma("D", T.fss[:], T.fs[:], "", "fss", "d_fs")
-    dma("D", T.pfs[:], T.pf[:], "", "pfs", "d_pf")
+    dma("S", T.pfs[:], T.pf[:], "", "pfs", "d_pf")
     dma("D", T.ths[:, 0:1], T.th[:], "", "ths", "d_th")
     dma("S", T.xfs[:, 0:4096], T.xf[:, 0:4096], "", "xfs", "d_xa")
     dma("D", T.xfs[:, 4096:8192], T.xf[:, 4096:8192], "", "xfsb", "d_xb")
@@ -183,13 +185,20 @@ def rank_program(g, core, T, topo):
     def gop(fn, R, W):
         op("G", fn, R, W)
     ms(T.ONES[:], 1.0, "ONES")
-    ms(T.SELP[:], 0.0, "SELP")
-    gop(lambda e: e.iota(T.IOTC[:], [[1, 512]], -256, 0, allow_small_or_imprecise_dtypes=True), "", "IOTC")
+    ms(T.NB[:, 0:1], -8.5, "NB")
     gop(lambda e: e.affine_select(T.SWT[:], T.ONES[:], [[-16, 8], [0, 16]], A.is_ge, 0.0, 0, 1), "ONES", "SWT")
     gop(lambda e: e.affine_select(T.G16[:], T.SWT[:], [[16, 8], [0, 16]], A.is_ge, 0.0, 15, -1), "SWT", "G16")
     gop(lambda e: e.affine_select(T.IDENT[:], T.ONES[:], [[-1, 128]], A.is_equal, 0.0, 0, 1), "ONES", "IDENT")
     gop(lambda e: e.iota(T.PI[:, 0:1], [[1, 1]], 0, 1), "", "PI")
     gop(lambda e: e.iota(T.LI[:], [[16, 16]], 0, 0), "", "LI")
+    for k in range(16):
+        gop(lambda e: e.affine_select(T.SELP[:, 128 * k:128 * k + 128], T.G16[:], [[0, 8], [1, 16]], A.is_equal, 0.0, -k, 0), "G16", "+SELP")
+    gop(lambda e: e.iota(T.IOTC[:], [[1, 512]], -256, 0, allow_small_or_imprecise_dtypes=True), "", "IOTC")
+    for b in range(9):
+        for c, v in ((b, 2 ** (8 - b)), (16 + b, 2 ** b if b else 0), (32 + b, -2 ** b if b else 1)):
+            gop(lambda e: e.iota(T.PAB[:, c:c + 1], [[0, 1]], v, 0, allow_small_or_imprecise_dtypes=True), "", "+PAB")
+    for x in ("XB0", "XB1"):
+        gop(lambda e: e.iota(T[x][:], [[0, WCOL]], 0, 0, allow_small_or_imprecise_dtypes=True), "", x)
     gop(lambda e: e.iota(T.IDX1[:], [[1, 256]], 1, 0, allow_small_or_imprecise_dtypes=True), "", "IDX1")
     for t in range(5):
         for c in (8, 536):
@@ -202,32 +211,43 @@ def rank_program(g, core, T, topo):
     act(T.CS[:], T.CBF[:].indirect(T.bsU[:]), "CBF bsU", "CS")
     for k in range(16):
         cp(T.F16[:, k::16], T.pfs[:], "pfs", "+F16")
-        act(T.N16[:, k::16], T.pns[:], "pns", "+N16")
-    cp(T.OA[:], T.CS[:].indirect(T.fsU[:]), "CS fsU", "OA")
     for k in range(16):
-        cp(T.SELP[:, 128 * k + k:128 * k + 128:16], T.G16[:, k::16], "G16", "+SELP")
+        cp(T.N16[:, k::16], T.pns[:], "pns", "+N16")
+    cp(T.OA[:], T.CS[:].indirect(T.fsU[:]), "CS fsU", "OA")
     ts(T.GN8[:], T.G16[:, ::16], -1.0, None, A.mult, None, "G16", "GN8")
-    for n, c in enumerate(NSET):
-        d, s = slice(512 * n, 512 * n + 512), slice(512 * c, 512 * c + 512)
-        ts(T.NNEG[:, d], T.N16[:, s], -1.0, None, A.mult, None, "N16", "+NNEG")
-        tt(T.FMN[:, d], T.F16[:, s], T.N16[:, s], A.subtract, "F16 N16", "+FMN")
-    for n, (bits, f, c) in enumerate(((4032, "thh", "THH"), (63, "thl", "THL"))):
+    for n, bits in enumerate((4032, 63)):
         op("V", lambda e: e.tensor_scalar(T.TI[:, n:n + 1], T.ths[:, 0:1], 1, bits, A.arith_shift_right, A.bitwise_and), "ths", "TI%d" % n)
-        cp(T[f][:, 0:1], T.TI[:, n:n + 1], "TI%d" % n, f)
-        ts(T[c][:], T.ONES[:], T[f][:, 0:1], -1.0, A.mult, A.mult, "ONES " + f, c)
+    for n in range(2):
+        cp(T.thh[:, n:n + 1], T.TI[:, n:n + 1], "TI%d" % n, "thh%d" % n)
+    for n, c in enumerate(("THH", "THL")):
+        ts(T[c][:], T.ONES[:], T.thh[:, n:n + 1], -1.0, A.mult, A.mult, "ONES thh%d" % n, c)
+
+    def setup_terms():
+        p = 32 * NSET[0]
+        tt(T.XN[:, 0:256 - p], T.pfs[:, p:256], T.pns[:, p:256], A.subtract, "pfs pns", "XN")
+        act(T.NNEG[:], T.N16[:, 16 * p:4096], "N16", "NNEG", scale=-1.0)
+        for k in range(16):
+            act(T.FMN[:, k::16], T.XN[:, 0:256 - p], "XN", "+FMN")
+        act(T.IDF[:], T.IDENT[:], "IDENT", "IDF")
+        act(T.NIDF[:], T.IDENT[:], "IDENT", "NIDF", scale=-1.0)
 
     def setup_lists():
         op("V", lambda e: e.tensor_scalar(T.PM[:, 0:1], T.PI[:, 0:1], 15, None, A.bitwise_and), "PI", "PM")
         cp(T.PMF[:, 0:1], T.PM[:, 0:1], "PM", "PMF")
         ts(T.LIF[:], T.LI[:], T.PMF[:, 0:1], None, A.add, None, "LI PMF", "LIF")
-        ts(T.BASE[:], T.LIF[:], 32.0, None, A.mult, None, "LIF", "BASE")
+        ts(T.BASE[:], T.LI[:], 32.0, None, A.mult, None, "LI", "BASE")
+        ts(T.PMF[:, 1:2], T.PM[:, 0:1], 32.0, None, A.mult, None, "PM", "PMF1")
         ts(T.LI1[:], T.LIF[:], 1.0, None, A.add, None, "LIF", "LI1")
         ts(T.AB0[:], T.LIF[:], 144.0, None, A.add, None, "LIF", "AB0")
         conv(T.PL[:, 0:16], T.pfs, 0, 16, "pfs", "PL")
-        cp(T.ELS[:], T.PL[:, 0:16], "PL", "ELS")
-        cp(T.MI0[:, 0:16], T.fss[:], "fss", "MI0")
         cp(T.BROW4[:].indirect(T.bsU[:]), T.IOTC[:], "IOTC bsU", "BROW4")
+        cp(T.MI0[:, 0:16], T.fss[:], "fss", "MI0")
+        cp(T.OI1[:], T.PL[:, 0:16], "PL", "OI1")
+        op("V", lambda e: e.tensor_scalar(T.OI2[:], T.OI1[:], 31, None, A.bitwise_and), "OI1", "OI2")
+        tt(T.ELS[:], T.OI2[:], T.BASE[:], A.add, "OI2 BASE", "ELS")
         act(T.GROW[:], T.BROW4[:].indirect(T.nbU[:]), "BROW4 nbU", "GROW")
+
+    def setup_sites():
         conv(T.PL[:, 16:32], T.GROW, 0, 16, "GROW", "PL")
         ts(T.MI0[:, 16:32], T.PL[:, 16:32], 0.0625, 256.0, A.mult, A.add, "PL", "MI0")
 
@@ -240,22 +260,17 @@ def rank_program(g, core, T, topo):
         ms(T.RTB[:], 1.0, "RTB")
         ts(T.LTB[:, 0:4], T.BITS[:, 0:4], -2.0, 1.0, A.mult, A.add, "BITS", "LTB")
         ts(T.RTB[:, 4:9], T.BITS[:, 4:9], -2.0, 1.0, A.mult, A.add, "BITS", "RTB")
-        for b in range(9):
-            ms(T.PAB[:, b:b + 1], float(2 ** (8 - b)), "+POW")
-            ms(T.PAB[:, 16 + b:17 + b], 2.0 ** b / 256 if b else 0.0, "+AC")
-            ms(T.PAB[:, 32 + b:33 + b], -2.0 ** (b - 1) if b else 0.5, "+BC")
-        ms(T.C128[:, 0:1], 1.0 / 128, "C128")
+        ms(T.C128[:, 0:1], 1.0 / 32768, "C128a")
+        ms(T.C128[:, 1:2], 1.0 / 256, "C128b")
         mm(T.PM2[0:9, 0:128], T.LTB[:, 0:9], T.IDENT[:], True, True, "LTB IDENT", "PM2")
         mm(T.PM2[0:9, 128:160], T.RTB[0:32, 0:9], T.IDENT[0:32, 0:32], True, True, "RTB IDENT", "PM2")
-        mm(T.PM2[0:9, 160:161], T.PAB[:, 16:25], T.C128[:, 0:1], True, True, "AC C128", "PM2")
-        mm(T.PM2[0:9, 161:162], T.PAB[:, 32:41], T.C128[:, 0:1], True, True, "BC C128", "PM2")
+        mm(T.PM2[0:9, 160:161], T.PAB[:, 16:25], T.C128[:, 0:1], True, True, "PAB C128a", "PM2")
+        mm(T.PM2[0:9, 161:162], T.PAB[:, 32:41], T.C128[:, 1:2], True, True, "PAB C128b", "PM2")
         cp(T.LB[0:9, :], T.PM2[0:9, 0:128], "PM2", "LB")
         cp(T.RC[0:9, :], T.PM2[0:9, 128:160], "PM2", "RC")
         cp(T.AB[0:9, 0:2], T.PM2[0:9, 160:162], "PM2", "AB")
 
     def setup_boxes():
-        ms(T.XB0[:], 0.0, "XB0")
-        ms(T.XB1[:], 0.0, "XB1")
         act(T.BROW[:], T.IOTC[:].indirect(T.bsU[:]), "IOTC bsU", "BROW")
         act(T.XB0[:, 144:400], T.BROW[:].indirect(T.fsU[:]), "BROW fsU", "XB0")
         act(T.XB0[:, 16:144], T.IOTC[:].indirect(T.nbU[:, 0:8]), "IOTC nbU", "XB0")
@@ -317,12 +332,15 @@ def rank_program(g, core, T, topo):
     def half_sum(h):
         cp(T.SW[:, 128 * h:128 * h + 128], T.PM2[:, 256:384], "PM2", "SW%d" % h)
         conv(T.PL[:, 8 * h:8 * h + 8], T.SW, 128 * h, 8, "SW%d" % h, "PL")
+        if h:
+            mm(T.PSC1[:, 128:384], T.G16[:], T.SW[:], True, True, "G16 SW0 SW1", "PSC1")
+            act(T.FLB[:], T.PSC1[:, 128:384], "PSC1 NB", "FLB", f=AF.Sign, bias=T.NB[:, 0:1])
 
     def half_rows(t, h):
         s = slice(128 * h, 128 * h + 128)
         wo, key = T["WO%d" % t], "WO%d%s" % (t, "ab"[h])
         p = T.PM2[:, 256:384]
-        tt(p, p, T.DD[:, s], A.mult, "DD%d PM2" % h, "PM2")
+        tt(p, T.PM2[:, s], T.SW[:, s], A.mult, "PM2 SW%d" % h, "PM2")
         a = slice(144 + 128 * h, 272 + 128 * h)
         hh = slice(16 + 384 * h, 144 + 384 * h)
         tt(wo[:, a], p, T.CAf[:, s], A.add, "PM2 CAf", "+" + key)
@@ -334,9 +352,8 @@ def rank_program(g, core, T, topo):
     def half_off(h):
         s = slice(8 * h, 8 * h + 8)
         tt(T.OI1[:, s], T.PL[:, s], T.ELS[:, s], A.add, "PL ELS", "OI1")
-        op("V", lambda e: e.tensor_scalar(T.OI2[:, s], T.OI1[:, s], 31, None, A.bitwise_and), "OI1", "OI2")
-        tt(T.OI3[:, s], T.OI2[:, s], T.BASE[:, s], A.add, "OI2 BASE", "OI3")
-        cp(T.OFFU[:, s], T.OI3[:, s], "OI3", "OFFU%d" % h)
+        op("V", lambda e: e.tensor_scalar(T.OI2[:, s], T.OI1[:, s], 8191 - 32, None, A.bitwise_and), "OI1", "OI2")
+        ts(T.OFFU[:, s], T.OI2[:, s], T.PMF[:, 1:2], None, A.add, None, "OI2 PMF1", "OFFU%d" % h)
 
     def half_put(h):
         s, r = slice(8 * h, 8 * h + 8), slice(128 * h, 128 * h + 128)
@@ -383,7 +400,8 @@ def rank_program(g, core, T, topo):
 
     def diff(h):
         s = slice(128 * h, 128 * h + 128)
-        tt(T.DD[:, s], T.CHf[:, s], T.CAf[:, s], A.subtract, "CAf CHf%d" % h, "DD%d" % h)
+        mm(T.PM2[:, s], T.IDF[:], T.CHf[:, s], True, False, "IDF CHf%d" % h, "PM2")
+        mm(T.PM2[:, s], T.NIDF[:], T.CAf[:, s], False, True, "NIDF CAf", "PM2")
 
     def sites_in(t):
         m = "MI%d" % t
@@ -392,23 +410,21 @@ def rank_program(g, core, T, topo):
 
     def chain(t):
         op("V", lambda e: e.tensor_reduce(T.RTOT[:, 0:1], T.PL[:, 0:16], AxisListType.X, A.add), "PL", "RTOT")
-        mm(T.PM2[0:9, 384:385], T.PAB[:, 0:9], T.RTOT[:, 0:1], True, True, "POW RTOT", "PM2")
+        mm(T.PM2[0:9, 384:385], T.PAB[:, 0:9], T.RTOT[:, 0:1], True, True, "PAB RTOT", "PM2")
         ts(T.TRN[:], T.PL[:, 0:16], 4.5, None, A.is_lt, None, "PL", "TRN")
         cp(T.UI[0:9, 0:1], T.PM2[0:9, 384:385], "PM2", "UI")
         op("V", lambda e: e.tensor_scalar(T.UB[0:9, 0:1], T.UI[0:9, 0:1], 256, None, A.bitwise_and), "UI", "UB")
         if t < 4:
             ts(T.FL16[:], T.PL[:, 0:16], 8.5, 0.0625, A.is_gt, A.mult, "PL", "FL16")
+        if t < 4:
+            take_h(t + 1, 0)
         ts(T.CF[0:9, 0:1], T.UB[0:9, 0:1], T.AB[0:9, 0:1], T.AB[0:9, 1:2], A.mult, A.add, "UB AB", "CF")
         tt(T.XX[:], T.TRN[:], T.DFG[:], A.mult, "TRN DFG", "XX")
         ts(T.RS[0:9, :], T.RC[0:9, :], T.CF[0:9, 0:1], None, A.mult, None, "RC CF", "RS")
         mm(T.PM2[:, 400:432], T.LB[0:9, :], T.RS[0:9, :], True, True, "LB RS", "PM2")
-        mm(T.PM2[:, 0:256], T.G16[:], T.SW[:], True, True, "G16 SW0 SW1", "PM2")
-        if t < 4:
-            take_h(t + 1, 0)
         m, mo = "MI%d" % t, "MO%d" % t
         tt(T[mo][:, 0:16], T[m][:, 0:16], T.XX[:], A.add, m + " XX", mo)
         ts(T.XLU[:], T.PM2[:, 400:432], 255.5, None, A.add, None, "PM2", "XLU")
-        ts(T.FLB[:], T.PM2[:, 0:256], 8.5, None, A.is_gt, None, "PM2", "FLB")
         tt(T.U[:, 0:512].indirect(T.FU[:]), T.FLB[:], T.IDX1[:], A.mult, "FLB IDX1 FU", "U0")
         if t < 4:
             tt(T[mo][:, 16:32], T[m][:, 16:32], T.XX[:], A.subtract, m + " XX", mo)
@@ -416,7 +432,7 @@ def rank_program(g, core, T, topo):
 
     def partner(t):
         act(T.U[:, 512:1024], T.U[:, 0:512].indirect(T.XLU[:]), "U0 XLU", "U1")
-        act(T.MROW[:], T.U[:, 512:1024].indirect(T.FU[:]), "U1 FU", "MROW")
+        act(T.MROW[:], T.U[:, 512:1024].indirect(T.FU[:]), "U1 FU", "MROW", f=AF.Relu)
         conv(T.PL[:, 32:48], T.MROW, 0, 16, "MROW", "PL")
 
     def alpha(t):
@@ -437,16 +453,12 @@ def rank_program(g, core, T, topo):
         act(T[b][:, 16:528], T[a][:].indirect(T.XLS[:]), a + " XLS", b)
 
     def box_lists():
-        conv(T.PL[:, 64:96], T.XB0, 16, 32, "XB0", "PL")
         ts(T.YL[:], T.PL[:, 64:96], 0.0625, 256.0, A.mult, A.add, "PL", "YL")
         cp(T.GU[:, 0:8], T.MI4[:, 16:24], "MI4", "GU")
         cp(T.GU[:, 8:24], T.MI4[:, 0:16], "MI4", "+GU")
         cp(T.GU[:, 24:32], T.MI4[:, 24:32], "MI4", "+GU")
-
-    def brow4():
         cp(T.BROW4[:].indirect(T.GU[:]), T.XB0[:, 16:528], "XB0 GU", "BROW4")
         conv(T.PL[:, 128:160], T.BROW4, 0, 32, "BROW4", "PL")
-        ts(T.BL[:], T.PL[:, 128:160], 0.0625, 256.0, A.mult, A.add, "PL", "BL")
 
     def put_yc(h):
         k = "WO4" + "ab"[h]
@@ -481,37 +493,43 @@ def rank_program(g, core, T, topo):
                 setup_xor()
             if j == 4 and t == 0:
                 setup_boxes()
-            if j == 5:
+                setup_sites()
+            if j == 7:
+                gop(lambda e: e.iota(T.U[:, 0:512], [[0, 512]], 0, 0, allow_small_or_imprecise_dtypes=True), "", "U0")
+            if j == 6 and t == 0:
+                setup_terms()
+            if j == 10:
                 floats(t, 0)
                 floats(t, 1)
             if j == 6 and t:
                 take_a(t)
                 st["oa"] = True
                 ahead(j)
-            if j == 9:
+            if j == JF:
                 floats(t, 2)
+            if j == 9:
                 sites_in(t)
-            if j == 13:
+            if j == JD:
                 diff(0)
-                diff(1)
             if t == 1 and j == 10:
-                boxes(0, T.MO0[:, 32:64], "MO0")
-            if t == 3 and j == 9:
+                boxes(0, T.MO0[:, 32:64], "MO0 MO0e0 MO0e1")
+            if t == 3 and j == 4:
                 boxes(1, T.HI1[:], "HI1")
-            if t == 3 and j == 11:
+            if t == 4 and j == 3:
                 boxes(2, T.HI2[:], "HI2")
             if t == 4 and j == 8:
                 boxes(3, T.MI4[:, 32:64], "MI4")
-            if t == 4 and j == 11:
-                box_lists()
             if t == 4 and j == 12:
-                brow4()
-            if j == 14:
+                conv(T.PL[:, 64:96], T.XB0, 16, 32, "XB0", "PL")
+            if t == 4 and j == 13:
+                box_lists()
+            if j == JC:
                 half_cmp(0)
             term_f(j)
-            if j == 14:
+            if j == JS:
                 half_sum(0)
                 half_rows(t, 0)
+                diff(1)
             term_n(j)
             if j < 12:
                 if j % 4 == 3:
@@ -519,7 +537,6 @@ def rank_program(g, core, T, topo):
                     lanes(j // 4, 1)
         lanes(3, 0)
         lanes(3, 1)
-        act(T.U[:, 0:512], T.IOTC[:], "IOTC", "U0", scale=0.0)
         half_eta(t, 0)
         if t < 4:
             half_off(0)
@@ -536,18 +553,23 @@ def rank_program(g, core, T, topo):
             put_yc(1)
             dma("D", T.yc[:], T.YC[:], "YC", "yc", "o_yc")
         half_eta(t, 1)
+        if t == 4:
+            ts(T.E4U[:, 0:8], T.WO4[:, 0:8], 16.0, None, A.add, None, "WO4e0", "E4U")
+            ts(T.E4U[:, 8:16], T.WO4[:, 528:536], 272.0, None, A.add, None, "WO4e1", "+E4U")
+            act(T.XN[:], T.XB0[:].indirect(T.E4U[:]), "XB0 E4U", "XN")
         chain(t)
 
     for t in range(5):
         main(t)
 
     dma("D", T.yf[:], T.MO4[:, 0:16], "MO4", "yf", "o_yf")
-    act(T.U[:, 512:1024], T.U[:, 0:512].indirect(T.XLU[:]), "U0 XLU", "U1")
+    conv(T.PL[:, 320:336], T.XN, 0, 16, "XN", "PL")
     act(T.U[:, 1024:1536], T.BROW4[:].indirect(T.XLU[:]), "BROW4 XLU", "U2")
+    act(T.U[:, 512:1024], T.U[:, 0:512].indirect(T.XLU[:]), "U0 XLU", "U1")
+    ts(T.Z3[:], T.PL[:, 320:336], 0.0625, 256.0, A.mult, A.add, "PL", "Z3")
+    dma("D", T.yn[:], T.Z3[:], "Z3", "yn", "o_yn")
+    ts(T.BL[:], T.PL[:, 128:160], 0.0625, 256.0, A.mult, A.add, "PL", "BL")
     conv(T.PL[:, 192:288], T.U, 0, 96, "U0 U1 U2", "PL")
-    ts(T.E4U[:, 0:8], T.WO4[:, 0:8], 16.0, None, A.add, None, "WO4e0", "E4U")
-    ts(T.E4U[:, 8:16], T.WO4[:, 528:536], 272.0, None, A.add, None, "WO4e1", "E4U")
-    act(T.XN[:], T.XB0[:].indirect(T.E4U[:]), "XB0 E4U", "XN")
     ts(T.B1[:], T.PL[:, 192:224], 0.5, None, A.is_gt, None, "PL", "B1")
     ts(T.B2[:], T.PL[:, 224:256], 0.5, None, A.is_gt, None, "PL", "B2")
     ts(T.B3[:], T.PL[:, 256:288], 0.0625, 256.0, A.mult, A.add, "PL", "B3")
@@ -556,9 +578,6 @@ def rank_program(g, core, T, topo):
     tt(T.B4[:], T.B3[:], T.B1[:], A.mult, "B3 B1", "B4")
     tt(T.YB[:], T.BL[:], T.B4[:], A.add, "BL B4", "YB")
     dma("D", T.yb[:], T.YB[:], "YB", "yb", "o_yb")
-    conv(T.PL[:, 320:336], T.XN, 0, 16, "XN", "PL")
-    ts(T.Z3[:], T.PL[:, 320:336], 0.0625, 256.0, A.mult, A.add, "PL", "Z3")
-    dma("D", T.yn[:], T.Z3[:], "Z3", "yn", "o_yn")
     for q in ("V", "S", "P", "G"):
         g.wait_ge(T.sem["q" + q], cnt[q])
     for n in ("yc", "yb", "yf", "yn"):

@@ -191,14 +191,15 @@ def rank_program(g, core, T, topo):
     gop(lambda e: e.affine_select(T.IDENT[:], T.ONES[:], [[-1, 128]], A.is_equal, 0.0, 0, 1), "ONES", "IDENT")
     gop(lambda e: e.iota(T.PI[:, 0:1], [[1, 1]], 0, 1), "", "PI")
     gop(lambda e: e.iota(T.LI[:], [[16, 16]], 0, 0), "", "LI")
+    gop(lambda e: e.iota(T.IOTC[:], [[1, 512]], -256, 0, allow_small_or_imprecise_dtypes=True), "", "IOTC")
+    for x in ("XB0", "XB1"):
+        for c in (0, 528):
+            gop(lambda e: e.iota(T[x][:, c:c + 16], [[0, 16]], 0, 0, allow_small_or_imprecise_dtypes=True), "", "+" + x)
     for k in range(16):
         gop(lambda e: e.affine_select(T.SELP[:, 128 * k:128 * k + 128], T.G16[:], [[0, 8], [1, 16]], A.is_equal, 0.0, -k, 0), "G16", "+SELP")
-    gop(lambda e: e.iota(T.IOTC[:], [[1, 512]], -256, 0, allow_small_or_imprecise_dtypes=True), "", "IOTC")
     for b in range(9):
         for c, v in ((b, 2 ** (8 - b)), (16 + b, 2 ** b if b else 0), (32 + b, -2 ** b if b else 1)):
             gop(lambda e: e.iota(T.PAB[:, c:c + 1], [[0, 1]], v, 0, allow_small_or_imprecise_dtypes=True), "", "+PAB")
-    for x in ("XB0", "XB1"):
-        gop(lambda e: e.iota(T[x][:], [[0, WCOL]], 0, 0, allow_small_or_imprecise_dtypes=True), "", x)
     gop(lambda e: e.iota(T.IDX1[:], [[1, 256]], 1, 0, allow_small_or_imprecise_dtypes=True), "", "IDX1")
     for t in range(5):
         for c in (8, 536):
@@ -209,6 +210,13 @@ def rank_program(g, core, T, topo):
     cp(T.CBF[:], T.cbs[:], "cbs", "CBF")
     cp(T.OH[:], T.CBF[:].indirect(T.nbU[:]), "CBF nbU", "OHa OHb")
     act(T.CS[:], T.CBF[:].indirect(T.bsU[:]), "CBF bsU", "CS")
+    p = 32 * NSET[0]
+    tt(T.XN[:, 0:256 - p], T.pfs[:, p:256], T.pns[:, p:256], A.subtract, "pfs pns", "XN")
+    for k in range(16):
+        act(T.NNEG[:, k::16], T.pns[:, p:256], "pns", "+NNEG", scale=-1.0)
+        act(T.FMN[:, k::16], T.XN[:, 0:256 - p], "XN", "+FMN")
+    act(T.IDF[:], T.IDENT[:], "IDENT", "IDF")
+    act(T.NIDF[:], T.IDENT[:], "IDENT", "NIDF", scale=-1.0)
     for k in range(16):
         cp(T.F16[:, k::16], T.pfs[:], "pfs", "+F16")
     for k in range(16):
@@ -222,15 +230,6 @@ def rank_program(g, core, T, topo):
     for n, c in enumerate(("THH", "THL")):
         ts(T[c][:], T.ONES[:], T.thh[:, n:n + 1], -1.0, A.mult, A.mult, "ONES thh%d" % n, c)
 
-    def setup_terms():
-        p = 32 * NSET[0]
-        tt(T.XN[:, 0:256 - p], T.pfs[:, p:256], T.pns[:, p:256], A.subtract, "pfs pns", "XN")
-        act(T.NNEG[:], T.N16[:, 16 * p:4096], "N16", "NNEG", scale=-1.0)
-        for k in range(16):
-            act(T.FMN[:, k::16], T.XN[:, 0:256 - p], "XN", "+FMN")
-        act(T.IDF[:], T.IDENT[:], "IDENT", "IDF")
-        act(T.NIDF[:], T.IDENT[:], "IDENT", "NIDF", scale=-1.0)
-
     def setup_lists():
         op("V", lambda e: e.tensor_scalar(T.PM[:, 0:1], T.PI[:, 0:1], 15, None, A.bitwise_and), "PI", "PM")
         cp(T.PMF[:, 0:1], T.PM[:, 0:1], "PM", "PMF")
@@ -239,16 +238,15 @@ def rank_program(g, core, T, topo):
         ts(T.PMF[:, 1:2], T.PM[:, 0:1], 32.0, None, A.mult, None, "PM", "PMF1")
         ts(T.LI1[:], T.LIF[:], 1.0, None, A.add, None, "LIF", "LI1")
         ts(T.AB0[:], T.LIF[:], 144.0, None, A.add, None, "LIF", "AB0")
-        conv(T.PL[:, 0:16], T.pfs, 0, 16, "pfs", "PL")
         cp(T.BROW4[:].indirect(T.bsU[:]), T.IOTC[:], "IOTC bsU", "BROW4")
         cp(T.MI0[:, 0:16], T.fss[:], "fss", "MI0")
+
+    def setup_sums():
         cp(T.OI1[:], T.PL[:, 0:16], "PL", "OI1")
         op("V", lambda e: e.tensor_scalar(T.OI2[:], T.OI1[:], 31, None, A.bitwise_and), "OI1", "OI2")
         tt(T.ELS[:], T.OI2[:], T.BASE[:], A.add, "OI2 BASE", "ELS")
-        act(T.GROW[:], T.BROW4[:].indirect(T.nbU[:]), "BROW4 nbU", "GROW")
 
     def setup_sites():
-        conv(T.PL[:, 16:32], T.GROW, 0, 16, "GROW", "PL")
         ts(T.MI0[:, 16:32], T.PL[:, 16:32], 0.0625, 256.0, A.mult, A.add, "PL", "MI0")
 
     def setup_xor():
@@ -262,10 +260,14 @@ def rank_program(g, core, T, topo):
         ts(T.RTB[:, 4:9], T.BITS[:, 4:9], -2.0, 1.0, A.mult, A.add, "BITS", "RTB")
         ms(T.C128[:, 0:1], 1.0 / 32768, "C128a")
         ms(T.C128[:, 1:2], 1.0 / 256, "C128b")
+
+    def setup_signs():
         mm(T.PM2[0:9, 0:128], T.LTB[:, 0:9], T.IDENT[:], True, True, "LTB IDENT", "PM2")
         mm(T.PM2[0:9, 128:160], T.RTB[0:32, 0:9], T.IDENT[0:32, 0:32], True, True, "RTB IDENT", "PM2")
         mm(T.PM2[0:9, 160:161], T.PAB[:, 16:25], T.C128[:, 0:1], True, True, "PAB C128a", "PM2")
         mm(T.PM2[0:9, 161:162], T.PAB[:, 32:41], T.C128[:, 1:2], True, True, "PAB C128b", "PM2")
+
+    def setup_signs2():
         cp(T.LB[0:9, :], T.PM2[0:9, 0:128], "PM2", "LB")
         cp(T.RC[0:9, :], T.PM2[0:9, 128:160], "PM2", "RC")
         cp(T.AB[0:9, 0:2], T.PM2[0:9, 160:162], "PM2", "AB")
@@ -416,8 +418,6 @@ def rank_program(g, core, T, topo):
         op("V", lambda e: e.tensor_scalar(T.UB[0:9, 0:1], T.UI[0:9, 0:1], 256, None, A.bitwise_and), "UI", "UB")
         if t < 4:
             ts(T.FL16[:], T.PL[:, 0:16], 8.5, 0.0625, A.is_gt, A.mult, "PL", "FL16")
-        if t < 4:
-            take_h(t + 1, 0)
         ts(T.CF[0:9, 0:1], T.UB[0:9, 0:1], T.AB[0:9, 0:1], T.AB[0:9, 1:2], A.mult, A.add, "UB AB", "CF")
         tt(T.XX[:], T.TRN[:], T.DFG[:], A.mult, "TRN DFG", "XX")
         ts(T.RS[0:9, :], T.RC[0:9, :], T.CF[0:9, 0:1], None, A.mult, None, "RC CF", "RS")
@@ -474,12 +474,14 @@ def rank_program(g, core, T, topo):
                 st["g"] += 1
             while st["p"] < min(st["g"], j + LP + 1, 16):
                 ident(st["p"])
+                if st["p"] in NS[0]:
+                    term_n(st["p"])
                 st["p"] += 1
         if t == 0:
             st["oh1"] = st["oa"] = True
         for j in range(16):
             ahead(j)
-            if j == 1 and t:
+            if j == 0 and t:
                 partner(t - 1)
             if j == 3 and t:
                 alpha(t - 1)
@@ -487,17 +489,18 @@ def rank_program(g, core, T, topo):
                 take_h(t, 1)
                 st["oh1"] = True
                 ahead(j)
-            if j == 2 and t == 0:
-                setup_lists()
-            if j == 3 and t == 0:
-                setup_xor()
-            if j == 4 and t == 0:
-                setup_boxes()
+            if t == 0 and j == 4:
+                conv(T.PL[:, 0:16], T.pfs, 0, 16, "pfs", "PL")
+                act(T.GROW[:], T.BROW4[:].indirect(T.nbU[:]), "BROW4 nbU", "GROW")
+            if t == 0 and j == 6:
+                setup_sums()
+                conv(T.PL[:, 16:32], T.GROW, 0, 16, "GROW", "PL")
+                setup_signs()
+            if t == 0 and j == 9:
                 setup_sites()
+                setup_signs2()
             if j == 7:
                 gop(lambda e: e.iota(T.U[:, 0:512], [[0, 512]], 0, 0, allow_small_or_imprecise_dtypes=True), "", "U0")
-            if j == 6 and t == 0:
-                setup_terms()
             if j == 10:
                 floats(t, 0)
                 floats(t, 1)
@@ -530,7 +533,8 @@ def rank_program(g, core, T, topo):
                 half_sum(0)
                 half_rows(t, 0)
                 diff(1)
-            term_n(j)
+            if j not in NS[0]:
+                term_n(j)
             if j < 12:
                 if j % 4 == 3:
                     lanes(j // 4, 0)
@@ -548,17 +552,22 @@ def rank_program(g, core, T, topo):
         half_rows(t, 1)
         if t < 4:
             half_off(1)
+            half_eta(t, 1)
             half_put(1)
         else:
+            half_eta(t, 1)
             put_yc(1)
             dma("D", T.yc[:], T.YC[:], "YC", "yc", "o_yc")
-        half_eta(t, 1)
-        if t == 4:
             ts(T.E4U[:, 0:8], T.WO4[:, 0:8], 16.0, None, A.add, None, "WO4e0", "E4U")
             ts(T.E4U[:, 8:16], T.WO4[:, 528:536], 272.0, None, A.add, None, "WO4e1", "+E4U")
             act(T.XN[:], T.XB0[:].indirect(T.E4U[:]), "XB0 E4U", "XN")
+        if t < 4:
+            take_h(t + 1, 0)
         chain(t)
 
+    setup_lists()
+    setup_boxes()
+    setup_xor()
     for t in range(5):
         main(t)
 
@@ -569,7 +578,9 @@ def rank_program(g, core, T, topo):
     ts(T.Z3[:], T.PL[:, 320:336], 0.0625, 256.0, A.mult, A.add, "PL", "Z3")
     dma("D", T.yn[:], T.Z3[:], "Z3", "yn", "o_yn")
     ts(T.BL[:], T.PL[:, 128:160], 0.0625, 256.0, A.mult, A.add, "PL", "BL")
-    conv(T.PL[:, 192:288], T.U, 0, 96, "U0 U1 U2", "PL")
+    conv(T.PL[:, 256:288], T.U, 1024, 32, "U2", "PL")
+    conv(T.PL[:, 192:224], T.U, 0, 32, "U0", "PL")
+    conv(T.PL[:, 224:256], T.U, 512, 32, "U1", "PL")
     ts(T.B1[:], T.PL[:, 192:224], 0.5, None, A.is_gt, None, "PL", "B1")
     ts(T.B2[:], T.PL[:, 224:256], 0.5, None, A.is_gt, None, "PL", "B2")
     ts(T.B3[:], T.PL[:, 256:288], 0.0625, 256.0, A.mult, A.add, "PL", "B3")

from concourse.mybir import AluOpType as A, AxisListType, ActivationFunctionType as AF

NS = ((), (5, 6, 7))
NSET = (5, 6, 7)
NXG, NT = 8, 2
LG = 7
JF, JD, JC, JS = 9, 14, 14, 14
LP = 2
WCOL = 544
FL, BF, I32, U16 = "float32", "bfloat16", "int32", "uint16"


def _scratch():
    s = {}

    def sb(names, cols, dt):
        for n in names.split():
            s[n] = ("sbuf", [128, cols], dt)
    sb("xfs", 8192, BF)
    sb("F16 N16", 4096, BF)
    sb("FMN NNEG", 512 * len(NSET), BF)
    sb("pfs pns FLB MROW IDX1 XN", 256, BF)
    sb("cbs", 512, I32)
    sb("CBF CS YC", 512, FL)
    sb("bss", 32, I32)
    sb("fss nbs OI1 OI2 BASE LI", 16, I32)
    sb("ths TI PI PM UI UB", 2, I32)
    sb("BITS", 16, I32)
    sb("IDF NIDF", 128, FL)
    sb("NB thh PMF RTOT CF AB C128", 2, FL)
    sb("ONES", 128, BF)
    sb("IDENT G16", 128, BF)
    sb("SELP", 2048, BF)
    sb("SWT THH THL", 128, BF)
    sb("GN8", 8, BF)
    sb("XG", 512 * NXG, BF)
    sb("TF TN", 2048 * NT, BF)
    sb("OH OA", 256, U16)
    sb("CAf CHf", 256, FL)
    sb("SW", 256, BF)
    sb("WI1 WI2 WI3 WI4 WO0 WO1 WO2 WO3 WO4", WCOL, FL)
    sb("MI0 MI1 MI2 MI3 MI4 MO0 MO1 MO2 MO3 MO4", 64, FL)
    sb("HI1 HI2", 32, FL)
    sb("bsU XLU XLS YL GU", 32, U16)
    sb("fsU nbU FU ETAU ALU OFFU E4U", 16, U16)
    sb("DFG TRN XX TD FL16 ABS Z1 Z2 Z3 LIF LI1 AB0 ELS", 16, FL)
    sb("U", 1536, BF)
    sb("IOTC BROW BROW4", 512, BF)
    sb("XB0 XB1", WCOL, BF)
    sb("GROW", 256, BF)
    sb("RS RC", 32, BF)
    sb("LB", 128, BF)
    sb("LTB RTB", 16, BF)
    sb("PAB", 48, FL)
    sb("BL B1 B2 B3 B4 YB", 32, FL)
    for n in ["PX0", "PX1", "PX2", "PX3", "PSC0", "PSC1", "PL", "PM2"]:
        s[n] = ("psum", [128, 512], FL)
    return s


SCRATCH = _scratch()
LOADS = ["pf", "pn", "fs", "bs", "nb", "th", "cb", "xa", "xb"]
SEMAPHORES = (["qV", "qS", "qP", "qG", "loc"] + ["d_" + n for n in LOADS] + ["o_yc", "o_yb", "o_yf", "o_yn"]
              + ["a%d_%d" % (k, t) for k in range(5) for t in range(1, 5)] + ["ah1", "ah2"])


def rank_program(g, core, T, topo):
    rank = T.rank_of(core)
    if rank is None:
        return
    N = len(T.cores)
    Q = {"V": g.vector, "S": g.scalar, "P": g.tensor, "G": g, "D": g.sync}
    cnt = {"V": 0, "S": 0, "P": 0, "G": 0}
    seen = {q: {} for q in Q}
    snap = {}
    wr, wp, rd = {}, {}, {}

    def need(q, R, W):
        toks = []
        for k in R:
            if k in wr:
                toks.append(wr[k])
            if k[0] == "P":
                toks += [t for qq, t in rd.get(k, {}).items() if qq != q]
        for k in W:
            w = wr if k[0] != "+" else wp
            k = k.lstrip("+")
            if k in w and (q != "P" or w[k][0] != "qP"):
                toks.append(w[k])
            toks += [t for qq, t in rd.get(k, {}).items() if q != "P" or qq != q]
        best = {}
        for s, v in toks:
            if v > seen[q].get(s, 0):
                best[s] = max(best.get(s, 0), v)
        for s in sorted(best, key=lambda s: -best[s]):
            v = best[s]
            if v <= seen[q].get(s, 0):
                continue
            Q[q].wait_ge(T.sem[s], v)
            for s2, v2 in snap.get((s, v), {}).items():
                seen[q][s2] = max(seen[q].get(s2, 0), v2)
            seen[q][s] = max(seen[q].get(s, 0), v)

    def done(q, R, W, tok):
        snap[tok] = dict(seen[q])
        for k in R:
            rd.setdefault(k, {})[q] = tok
        for k in W:
            wr[k.lstrip("+")] = tok
            if k[0] != "+":
                wp[k] = tok
                rd[k] = {}

    def op(q, fn, R, W):
        R, W = R.split(), W.split()
        need(q, R, W)
        fn(Q[q]).then_inc(T.sem["q" + q], 1)
        cnt[q] += 1
        done(q, R, W, ("q" + q, cnt[q]))

    def dma(q, out, in_, R, W, sem):
        R, W = R.split(), W.split()
        need(q, R, W)
        Q[q].dma_start(out, in_).then_inc(T.sem[sem], 16)
        done(q, R, W, (sem, 16))

    nloc = [0]

    def send(dst, out, in_, R, sem):
        need("G", R.split(), [])
        m = topo.mask(core, dst)
        rid, pid, _s = topo.addr(dst)
        g.remote_dma(out, in_, T.sem[sem], T.sem.loc, pid, rid, m)
        nloc[0] += len(topo.engines(core, dst))

    for t in range(1, 5):
        src = T.cores[(rank - 1) % N]
        ne = len(topo.engines(src, core))
        wr["WI%da" % t] = ("a0_%d" % t, ne)
        wr["WI%db" % t] = ("a1_%d" % t, ne)
        wr["WI%de0" % t] = ("a3_%d" % t, ne)
        wr["WI%de1" % t] = ("a4_%d" % t, ne)
        wr["MI%d" % t] = ("a2_%d" % t, ne)
    wr["HI1"] = ("ah1", len(topo.engines(T.cores[(rank + 1) % N], core)))
    wr["HI2"] = ("ah2", len(topo.engines(T.cores[(rank + 2) % N], core)))

    def tt(o, a, b, o_, R, W):
        op("V", lambda e: e.tensor_tensor(o, a, b, o_), R, W)

    def ts(o, a, s1, s2, o0, o1, R, W):
        if o1 is None:
            op("V", lambda e: e.tensor_scalar(o, a, s1, None, o0), R, W)
        else:
            op("V", lambda e: e.tensor_scalar(o, a, s1, s2, o0, o1), R, W)

    def cp(o, a, R, W):
        op("V", lambda e: e.tensor_copy(o, a), R, W)

    def ms(o, c, W):
        op("V", lambda e: e.memset(o, c), "", W)

    def act(o, a, R, W, f=AF.Copy, **kw):
        op("S", lambda e: e.activation(o, a, f, **kw), R, W)

    def mm(o, l, r, st, sp, R, W):
        op("P", lambda e: e.matmul(o, l, r, st, sp), R, W)

    def sel(k):
        return T.SELP[:, 128 * k:128 * k + 128]

    def conv(out, row, a, n, R, W):
        for l in range(16):
            mm(out, sel(l), row[:, a + l:a + 16 * (n - 1) + l + 1:16], l == 0, l == 15, R + " SELP", W)

    dma("D", T.nbs[:], T.nb[:], "", "nbs", "d_nb")
    dma("S", T.cbs[:], T.cb[:], "", "cbs", "d_cb")
    dma("D", T.bss[:], T.bs[:], "", "bss", "d_bs")
    dma("S", T.pns[:], T.pn[:], "", "pns", "d_pn")
    dma("D", T.fss[:], T.fs[:], "", "fss", "d_fs")
    dma("S", T.pfs[:], T.pf[:], "", "pfs", "d_pf")
    dma("D", T.ths[:, 0:1], T.th[:], "", "ths", "d_th")
    dma("S", T.xfs[:, 0:4096], T.xf[:, 0:4096], "", "xfs", "d_xa")
    dma("D", T.xfs[:, 4096:8192], T.xf[:, 4096:8192], "", "xfsb", "d_xb")

    def gop(fn, R, W):
        op("G", fn, R, W)
    ms(T.ONES[:], 1.0, "ONES")
    ms(T.NB[:, 0:1], -8.5, "NB")
    gop(lambda e: e.affine_select(T.SWT[:], T.ONES[:], [[-16, 8], [0, 16]], A.is_ge, 0.0, 0, 1), "ONES", "SWT")
    gop(lambda e: e.affine_select(T.G16[:], T.SWT[:], [[16, 8], [0, 16]], A.is_ge, 0.0, 15, -1), "SWT", "G16")
    gop(lambda e: e.affine_select(T.IDENT[:], T.ONES[:], [[-1, 128]], A.is_equal, 0.0, 0, 1), "ONES", "IDENT")
    gop(lambda e: e.iota(T.PI[:, 0:1], [[1, 1]], 0, 1), "", "PI")
    gop(lambda e: e.iota(T.LI[:], [[16, 16]], 0, 0), "", "LI")
    gop(lambda e: e.iota(T.IOTC[:], [[1, 512]], -256, 0, allow_small_or_imprecise_dtypes=True), "", "IOTC")
    for x in ("XB0", "XB1"):
        for c in (0, 528):
            gop(lambda e: e.iota(T[x][:, c:c + 16], [[0, 16]], 0, 0, allow_small_or_imprecise_dtypes=True), "", "+" + x)
    for k in range(16):
        gop(lambda e: e.affine_select(T.SELP[:, 128 * k:128 * k + 128], T.G16[:], [[0, 8], [1, 16]], A.is_equal, 0.0, -k, 0), "G16", "+SELP")
    for b in range(9):
        for c, v in ((b, 2 ** (8 - b)), (16 + b, 2 ** b if b else 0), (32 + b, -2 ** b if b else 1)):
            gop(lambda e: e.iota(T.PAB[:, c:c + 1], [[0, 1]], v, 0, allow_small_or_imprecise_dtypes=True), "", "+PAB")
    gop(lambda e: e.iota(T.IDX1[:], [[1, 256]], 1, 0, allow_small_or_imprecise_dtypes=True), "", "IDX1")
    for t in range(5):
        for c in (8, 536):
            gop(lambda e: e.iota(T["WO%d" % t][:, c:c + 8], [[0, 8]], 0, 0, allow_small_or_imprecise_dtypes=True), "", "WO%dp" % t)
    cp(T.fsU[:], T.fss[:], "fss", "fsU")
    cp(T.bsU[:], T.bss[:], "bss", "bsU")
    cp(T.nbU[:], T.nbs[:], "nbs", "nbU")
    cp(T.CBF[:], T.cbs[:], "cbs", "CBF")
    cp(T.OH[:], T.CBF[:].indirect(T.nbU[:]), "CBF nbU", "OHa OHb")
    act(T.CS[:], T.CBF[:].indirect(T.bsU[:]), "CBF bsU", "CS")
    p = 32 * NSET[0]
    tt(T.XN[:, 0:256 - p], T.pfs[:, p:256], T.pns[:, p:256], A.subtract, "pfs pns", "XN")
    for k in range(16):
        act(T.NNEG[:, k::16], T.pns[:, p:256], "pns", "+NNEG", scale=-1.0)
        act(T.FMN[:, k::16], T.XN[:, 0:256 - p], "XN", "+FMN")
    act(T.IDF[:], T.IDENT[:], "IDENT", "IDF")
    act(T.NIDF[:], T.IDENT[:], "IDENT", "NIDF", scale=-1.0)
    for k in range(16):
        cp(T.F16[:, k::16], T.pfs[:], "pfs", "+F16")
    for k in range(16):
        cp(T.N16[:, k::16], T.pns[:], "pns", "+N16")
    cp(T.OA[:], T.CS[:].indirect(T.fsU[:]), "CS fsU", "OA")
    ts(T.GN8[:], T.G16[:, ::16], -1.0, None, A.mult, None, "G16", "GN8")
    for n, bits in enumerate((4032, 63)):
        op("V", lambda e: e.tensor_scalar(T.TI[:, n:n + 1], T.ths[:, 0:1], 1, bits, A.arith_shift_right, A.bitwise_and), "ths", "TI%d" % n)
    for n in range(2):
        cp(T.thh[:, n:n + 1], T.TI[:, n:n + 1], "TI%d" % n, "thh%d" % n)
    for n, c in enumerate(("THH", "THL")):
        ts(T[c][:], T.ONES[:], T.thh[:, n:n + 1], -1.0, A.mult, A.mult, "ONES thh%d" % n, c)

    def setup_lists():
        op("V", lambda e: e.tensor_scalar(T.PM[:, 0:1], T.PI[:, 0:1], 15, None, A.bitwise_and), "PI", "PM")
        cp(T.PMF[:, 0:1], T.PM[:, 0:1], "PM", "PMF")
        ts(T.LIF[:], T.LI[:], T.PMF[:, 0:1], None, A.add, None, "LI PMF", "LIF")
        ts(T.BASE[:], T.LI[:], 32.0, None, A.mult, None, "LI", "BASE")
        ts(T.PMF[:, 1:2], T.PM[:, 0:1], 32.0, None, A.mult, None, "PM", "PMF1")
        ts(T.LI1[:], T.LIF[:], 1.0, None, A.add, None, "LIF", "LI1")
        ts(T.AB0[:], T.LIF[:], 144.0, None, A.add, None, "LIF", "AB0")
        cp(T.BROW4[:].indirect(T.bsU[:]), T.IOTC[:], "IOTC bsU", "BROW4")
        cp(T.MI0[:, 0:16], T.fss[:], "fss", "MI0")

    def setup_sums():
        cp(T.OI1[:], T.PL[:, 0:16], "PL", "OI1")
        op("V", lambda e: e.tensor_scalar(T.OI2[:], T.OI1[:], 31, None, A.bitwise_and), "OI1", "OI2")
        tt(T.ELS[:], T.OI2[:], T.BASE[:], A.add, "OI2 BASE", "ELS")

    def setup_sites():
        ts(T.MI0[:, 16:32], T.PL[:, 16:32], 0.0625, 256.0, A.mult, A.add, "PL", "MI0")

    def setup_xor():
        for b in range(4):
            op("V", lambda e: e.tensor_scalar(T.BITS[:, b:b + 1], T.PM[:, 0:1], b, 1, A.arith_shift_right, A.bitwise_and), "PM", "+BITS")
        for b in range(5):
            op("V", lambda e: e.tensor_scalar(T.BITS[:, 4 + b:5 + b], T.PI[:, 0:1], b, 1, A.arith_shift_right, A.bitwise_and), "PI", "+BITS")
        ms(T.LTB[:], 1.0, "LTB")
        ms(T.RTB[:], 1.0, "RTB")
        ts(T.LTB[:, 0:4], T.BITS[:, 0:4], -2.0, 1.0, A.mult, A.add, "BITS", "LTB")
        ts(T.RTB[:, 4:9], T.BITS[:, 4:9], -2.0, 1.0, A.mult, A.add, "BITS", "RTB")
        ms(T.C128[:, 0:1], 1.0 / 32768, "C128a")
        ms(T.C128[:, 1:2], 1.0 / 256, "C128b")

    def setup_signs():
        mm(T.PM2[0:9, 0:128], T.LTB[:, 0:9], T.IDENT[:], True, True, "LTB IDENT", "PM2")
        mm(T.PM2[0:9, 128:160], T.RTB[0:32, 0:9], T.IDENT[0:32, 0:32], True, True, "RTB IDENT", "PM2")
        mm(T.PM2[0:9, 160:161], T.PAB[:, 16:25], T.C128[:, 0:1], True, True, "PAB C128a", "PM2")
        mm(T.PM2[0:9, 161:162], T.PAB[:, 32:41], T.C128[:, 1:2], True, True, "PAB C128b", "PM2")

    def setup_signs2():
        cp(T.LB[0:9, :], T.PM2[0:9, 0:128], "PM2", "LB")
        cp(T.RC[0:9, :], T.PM2[0:9, 128:160], "PM2", "RC")
        cp(T.AB[0:9, 0:2], T.PM2[0:9, 160:162], "PM2", "AB")

    def setup_boxes():
        act(T.BROW[:], T.IOTC[:].indirect(T.bsU[:]), "IOTC bsU", "BROW")
        act(T.XB0[:, 144:400], T.BROW[:].indirect(T.fsU[:]), "BROW fsU", "XB0")
        act(T.XB0[:, 16:144], T.IOTC[:].indirect(T.nbU[:, 0:8]), "IOTC nbU", "XB0")
        act(T.XB0[:, 400:528], T.IOTC[:].indirect(T.nbU[:, 8:16]), "IOTC nbU", "XB0")

    def xg(j):
        return T.XG[:, 512 * (j % NXG):512 * (j % NXG) + 512]

    def gather(j):
        off = T.OH if j < 8 else T.OA
        key = ("OHa" if j < 4 else "OHb") if j < 8 else "OA"
        c = j % 8
        act(xg(j), T.xfs[:].indirect(off[:, 32 * c:32 * c + 32]), "xfs xfsb " + key, "XG%d" % (j % NXG))

    def ident(j):
        c, b = j % 8, "PX%d" % (j % 4)
        x = "XG%d" % (j % NXG)
        if c in NS[j // 8]:
            n = NSET.index(c)
            mm(T[b][:], T.IDENT[:], xg(j), True, False, "IDENT " + x, b)
            mm(T[b][:], T.IDENT[:], T.NNEG[:, 512 * n:512 * n + 512], False, True, "IDENT NNEG", b)
        else:
            mm(T[b][:], T.IDENT[:], xg(j), True, True, "IDENT " + x, b)

    def term_f(j):
        c, b, n = j % 8, "PX%d" % (j % 4), (j // 4) % NT
        o = T.TF[:, 512 * (j % 8):512 * (j % 8) + 512]
        if c in NS[j // 8]:
            tab, key, a = T.FMN, "FMN", NSET.index(c)
        else:
            tab, key, a = T.F16, "F16", c
        tt(o, T[b][:], tab[:, 512 * a:512 * a + 512], A.max, b + " " + key, "TF%d_%d" % (n, j % 4))

    def term_n(j):
        c, b, n = j % 8, "PX%d" % (j % 4), (j // 4) % NT
        o = T.TN[:, 512 * (j % 8):512 * (j % 8) + 512]
        if c in NS[j // 8]:
            act(o, T[b][:], b, "TN%d_%d" % (n, j % 4), f=AF.Relu)
        else:
            tt(o, T[b][:], T.N16[:, 512 * c:512 * c + 512], A.max, b + " N16", "TN%d_%d" % (n, j % 4))

    def lanes(blk, which):
        a, h = blk >= 2, blk % 2
        nm = "%s%d" % (("TF", "TN")[which], blk % NT)
        P = "PSC%d" % h
        if not a and which == 0:
            mm(T[P][:, 0:128], T.THH[:], T.IDENT[:], True, False, "THH IDENT", P)
            mm(T[P][:, 0:128], T.THL[:], T.IDENT[:], False, False, "THL IDENT", P)
        tab, key = (T.G16[:, ::16], "G16") if a == (which == 0) else (T.GN8[:], "GN8")
        for k in range(16):
            o = 2048 * (blk % NT)
            mm(T[P][:, k:128:16], T[nm[0:2]][:, o + k:o + 2048:16], tab, False, a and which == 1 and k == 15,
               "%s_0 %s_1 %s_2 %s_3 %s" % (nm, nm, nm, nm, key), P)

    def half_cmp(h):
        ts(T.SWT[:], T["PSC%d" % h][:, 0:128], 0.0, None, A.is_gt, None, "PSC%d" % h, "SWT")
        mm(T.PM2[:, 256:384], T.SWT[:], T.IDENT[:], True, True, "SWT IDENT", "PM2")

    def half_sum(h):
        cp(T.SW[:, 128 * h:128 * h + 128], T.PM2[:, 256:384], "PM2", "SW%d" % h)
        conv(T.PL[:, 8 * h:8 * h + 8], T.SW, 128 * h, 8, "SW%d" % h, "PL")
        if h:
            mm(T.PSC1[:, 128:384], T.G16[:], T.SW[:], True, True, "G16 SW0 SW1", "PSC1")
            act(T.FLB[:], T.PSC1[:, 128:384], "PSC1 NB", "FLB", f=AF.Sign, bias=T.NB[:, 0:1])

    def half_rows(t, h):
        s = slice(128 * h, 128 * h + 128)
        wo, key = T["WO%d" % t], "WO%d%s" % (t, "ab"[h])
        p = T.PM2[:, 256:384]
        tt(p, T.PM2[:, s], T.SW[:, s], A.mult, "PM2 SW%d" % h, "PM2")
        a = slice(144 + 128 * h, 272 + 128 * h)
        hh = slice(16 + 384 * h, 144 + 384 * h)
        tt(wo[:, a], p, T.CAf[:, s], A.add, "PM2 CAf", "+" + key)
        tt(wo[:, hh], T.CHf[:, s], p, A.subtract, "PM2 CHf%d" % h, "+" + key)
        if t < 4:
            w = slice(16 + 256 * h, 272 + 256 * h)
            send(T.cores[(rank + 1) % N], T["WI%d" % (t + 1)][:, w], wo[:, w], key, "a%d_%d" % (h, t + 1))

    def half_off(h):
        s = slice(8 * h, 8 * h + 8)
        tt(T.OI1[:, s], T.PL[:, s], T.ELS[:, s], A.add, "PL ELS", "OI1")
        op("V", lambda e: e.tensor_scalar(T.OI2[:, s], T.OI1[:, s], 8191 - 32, None, A.bitwise_and), "OI1", "OI2")
        ts(T.OFFU[:, s], T.OI2[:, s], T.PMF[:, 1:2], None, A.add, None, "OI2 PMF1", "OFFU%d" % h)

    def half_put(h):
        s, r = slice(8 * h, 8 * h + 8), slice(128 * h, 128 * h + 128)
        cp(T.xfs[:].indirect(T.OFFU[:, s]), T.pfs[:, r], "pfs OFFU%d" % h, "xfs xfsb")

    def half_eta(t, h):
        s = slice(8 * h, 8 * h + 8)
        wo, key = T["WO%d" % t], "WO%d%s" % (t, "ab"[h])
        e = slice(528 * h, 528 * h + 16)
        ts(T.TD[:, s], T.PL[:, s], 4.5, (-128.0, 128.0)[h], A.is_lt, A.mult, "PL", "TD%d" % h)
        tt(wo[:, 528 * h:528 * h + 8], T.LIF[:, s], T.TD[:, s], A.subtract, "LIF TD%d" % h, "WO%de%d" % (t, h))
        if t < 4:
            send(T.cores[(rank + 1) % N], T["WI%d" % (t + 1)][:, e], wo[:, e], "WO%de%d WO%dp" % (t, h, t), "a%d_%d" % (3 + h, t + 1))
            act(T["MO%d" % t][:, 32 + 24 * h:40 + 24 * h], wo[:, 528 * h:528 * h + 8], "WO%de%d" % (t, h), "MO%de%d" % (t, h),
                f=AF.Identity, bias=(16.0, 272.0)[h])

    def win(t, h):
        return T["WI%d" % t][:, 16 + 256 * h:272 + 256 * h]

    def take_h(t, h):
        s = slice(8 * h, 8 * h + 8)
        cp(T.ETAU[:, s], T["WI%d" % t][:, 528 * h:528 * h + 8], "WI%de%d" % (t, h), "ETAU%d" % h)
        cp(T.OH[:, 128 * h:128 * h + 128], win(t, h).indirect(T.ETAU[:, s]), "WI%d%s ETAU%d" % (t, "ab"[h], h), "OH" + "ab"[h])

    def all_in(t):
        return "WI%da WI%db WI%de0 WI%de1 " % (t, t, t, t)

    def take_a(t):
        cp(T.ALU[:], T["MI%d" % t][:, 40:56], "MI%d" % t, "ALU")
        cp(T.OA[:], T["WI%d" % t][:].indirect(T.ALU[:]), all_in(t) + "ALU", "OA")

    def floats(t, part):
        if t == 0:
            if part < 2:
                h = part
                act(T.CHf[:, 128 * h:128 * h + 128], T.CBF[:].indirect(T.nbU[:, 8 * h:8 * h + 8]), "CBF nbU", "CHf%d" % h)
            else:
                act(T.CAf[:], T.CS[:].indirect(T.fsU[:]), "CS fsU", "CAf")
        elif part < 2:
            h = part
            act(T.CHf[:, 128 * h:128 * h + 128], win(t, h).indirect(T.ETAU[:, 8 * h:8 * h + 8]), "WI%d%s ETAU%d" % (t, "ab"[h], h), "CHf%d" % h)
        else:
            act(T.CAf[:], T["WI%d" % t][:].indirect(T.ALU[:]), all_in(t) + "ALU", "CAf")

    def diff(h):
        s = slice(128 * h, 128 * h + 128)
        mm(T.PM2[:, s], T.IDF[:], T.CHf[:, s], True, False, "IDF CHf%d" % h, "PM2")
        mm(T.PM2[:, s], T.NIDF[:], T.CAf[:, s], False, True, "NIDF CAf", "PM2")

    def sites_in(t):
        m = "MI%d" % t
        cp(T.FU[:], T[m][:, 0:16], m, "FU")
        tt(T.DFG[:], T[m][:, 16:32], T[m][:, 0:16], A.subtract, m, "DFG")

    def chain(t):
        op("V", lambda e: e.tensor_reduce(T.RTOT[:, 0:1], T.PL[:, 0:16], AxisListType.X, A.add), "PL", "RTOT")
        mm(T.PM2[0:9, 384:385], T.PAB[:, 0:9], T.RTOT[:, 0:1], True, True, "PAB RTOT", "PM2")
        ts(T.TRN[:], T.PL[:, 0:16], 4.5, None, A.is_lt, None, "PL", "TRN")
        cp(T.UI[0:9, 0:1], T.PM2[0:9, 384:385], "PM2", "UI")
        op("V", lambda e: e.tensor_scalar(T.UB[0:9, 0:1], T.UI[0:9, 0:1], 256, None, A.bitwise_and), "UI", "UB")
        if t < 4:
            ts(T.FL16[:], T.PL[:, 0:16], 8.5, 0.0625, A.is_gt, A.mult, "PL", "FL16")
        ts(T.CF[0:9, 0:1], T.UB[0:9, 0:1], T.AB[0:9, 0:1], T.AB[0:9, 1:2], A.mult, A.add, "UB AB", "CF")
        tt(T.XX[:], T.TRN[:], T.DFG[:], A.mult, "TRN DFG", "XX")
        ts(T.RS[0:9, :], T.RC[0:9, :], T.CF[0:9, 0:1], None, A.mult, None, "RC CF", "RS")
        mm(T.PM2[:, 400:432], T.LB[0:9, :], T.RS[0:9, :], True, True, "LB RS", "PM2")
        m, mo = "MI%d" % t, "MO%d" % t
        tt(T[mo][:, 0:16], T[m][:, 0:16], T.XX[:], A.add, m + " XX", mo)
        ts(T.XLU[:], T.PM2[:, 400:432], 255.5, None, A.add, None, "PM2", "XLU")
        tt(T.U[:, 0:512].indirect(T.FU[:]), T.FLB[:], T.IDX1[:], A.mult, "FLB IDX1 FU", "U0")
        if t < 4:
            tt(T[mo][:, 16:32], T[m][:, 16:32], T.XX[:], A.subtract, m + " XX", mo)
            tt(T.ABS[:], T.AB0[:], T.TD[:], A.add, "AB0 TD0 TD1", "ABS")

    def partner(t):
        act(T.U[:, 512:1024], T.U[:, 0:512].indirect(T.XLU[:]), "U0 XLU", "U1")
        act(T.MROW[:], T.U[:, 512:1024].indirect(T.FU[:]), "U1 FU", "MROW", f=AF.Relu)
        conv(T.PL[:, 32:48], T.MROW, 0, 16, "MROW", "PL")

    def alpha(t):
        mo = "MO%d" % t
        tt(T.Z1[:], T.PL[:, 32:48], T.FL16[:], A.mult, "PL FL16", "Z1")
        ts(T.Z2[:], T.Z1[:], 256.0, None, A.mult, None, "Z1", "Z2")
        tt(T.Z1[:], T.Z1[:], T.ABS[:], A.add, "Z1 ABS", "Z1")
        tt(T.Z3[:], T.Z2[:], T.LI1[:], A.min, "Z2 LI1", "Z3")
        tt(T[mo][:, 40:56], T.Z1[:], T.Z3[:], A.subtract, "Z1 Z3", mo)
        mo += " %se0 %se1" % (mo, mo)
        send(T.cores[(rank + 1) % N], T["MI%d" % (t + 1)][:], T["MO%d" % t][:], mo, "a2_%d" % (t + 1))
        if t in (1, 2):
            send(T.cores[(rank - t) % N], T["HI%d" % t][:], T["MO%d" % t][:, 32:64], mo, "ah%d" % t)

    def boxes(n, lists, key):
        a, b = "XB%d" % (n % 2), "XB%d" % (1 - n % 2)
        cp(T.XLS[:], lists, key, "XLS")
        act(T[b][:, 16:528], T[a][:].indirect(T.XLS[:]), a + " XLS", b)

    def box_lists():
        ts(T.YL[:], T.PL[:, 64:96], 0.0625, 256.0, A.mult, A.add, "PL", "YL")
        cp(T.GU[:, 0:8], T.MI4[:, 16:24], "MI4", "GU")
        cp(T.GU[:, 8:24], T.MI4[:, 0:16], "MI4", "+GU")
        cp(T.GU[:, 24:32], T.MI4[:, 24:32], "MI4", "+GU")
        cp(T.BROW4[:].indirect(T.GU[:]), T.XB0[:, 16:528], "XB0 GU", "BROW4")
        conv(T.PL[:, 128:160], T.BROW4, 0, 32, "BROW4", "PL")

    def put_yc(h):
        k = "WO4" + "ab"[h]
        cp(T.YC[:].indirect(T.YL[:, 16 * h:16 * h + 16]), T.WO4[:, 16 + 256 * h:272 + 256 * h], k + " YL", "YC")

    def main(t):
        st = {"g": 0, "p": 0}

        def ahead(j):
            lim = 4 if not st.get("oh1") else (8 if not st.get("oa") else 16)
            while st["g"] < min(lim, j + LG if j else 3):
                gather(st["g"])
                st["g"] += 1
            while st["p"] < min(st["g"], j + LP + 1, 16):
                ident(st["p"])
                if st["p"] in NS[0]:
                    term_n(st["p"])
                st["p"] += 1
        if t == 0:
            st["oh1"] = st["oa"] = True
        for j in range(16):
            ahead(j)
            if j == 0 and t:
                partner(t - 1)
            if j == 3 and t:
                alpha(t - 1)
            if j == 2 and t:
                take_h(t, 1)
                st["oh1"] = True
                ahead(j)
            if t == 0 and j == 4:
                conv(T.PL[:, 0:16], T.pfs, 0, 16, "pfs", "PL")
                act(T.GROW[:], T.BROW4[:].indirect(T.nbU[:]), "BROW4 nbU", "GROW")
            if t == 0 and j == 6:
                setup_sums()
                conv(T.PL[:, 16:32], T.GROW, 0, 16, "GROW", "PL")
                setup_signs()
            if t == 0 and j == 9:
                setup_sites()
                setup_signs2()
            if j == 7:
                gop(lambda e: e.iota(T.U[:, 0:512], [[0, 512]], 0, 0, allow_small_or_imprecise_dtypes=True), "", "U0")
            if j == 10:
                floats(t, 0)
                floats(t, 1)
            if j == 6 and t:
                take_a(t)
                st["oa"] = True
                ahead(j)
            if j == JF:
                floats(t, 2)
            if j == 9:
                sites_in(t)
            if j == JD:
                diff(0)
            if t == 1 and j == 10:
                boxes(0, T.MO0[:, 32:64], "MO0 MO0e0 MO0e1")
            if t == 3 and j == 4:
                boxes(1, T.HI1[:], "HI1")
            if t == 4 and j == 3:
                boxes(2, T.HI2[:], "HI2")
            if t == 4 and j == 8:
                boxes(3, T.MI4[:, 32:64], "MI4")
            if t == 4 and j == 12:
                conv(T.PL[:, 64:96], T.XB0, 16, 32, "XB0", "PL")
            if t == 4 and j == 13:
                box_lists()
            if j == JC:
                half_cmp(0)
            term_f(j)
            if j == JS:
                half_sum(0)
                half_rows(t, 0)
                diff(1)
            if j not in NS[0]:
                term_n(j)
            if j < 12:
                if j % 4 == 3:
                    lanes(j // 4, 0)
                    lanes(j // 4, 1)
        lanes(3, 0)
        lanes(3, 1)
        half_eta(t, 0)
        if t < 4:
            half_off(0)
            half_put(0)
        else:
            put_yc(0)
        half_cmp(1)
        half_sum(1)
        half_rows(t, 1)
        if t < 4:
            half_off(1)
            half_eta(t, 1)
            half_put(1)
        else:
            half_eta(t, 1)
            put_yc(1)
            dma("D", T.yc[:], T.YC[:], "YC", "yc", "o_yc")
            ts(T.E4U[:, 0:8], T.WO4[:, 0:8], 16.0, None, A.add, None, "WO4e0", "E4U")
            ts(T.E4U[:, 8:16], T.WO4[:, 528:536], 272.0, None, A.add, None, "WO4e1", "+E4U")
            act(T.XN[:], T.XB0[:].indirect(T.E4U[:]), "XB0 E4U", "XN")
        if t < 4:
            take_h(t + 1, 0)
        chain(t)

    setup_lists()
    setup_boxes()
    setup_xor()
    for t in range(5):
        main(t)

    dma("D", T.yf[:], T.MO4[:, 0:16], "MO4", "yf", "o_yf")
    conv(T.PL[:, 320:336], T.XN, 0, 16, "XN", "PL")
    act(T.U[:, 1024:1536], T.BROW4[:].indirect(T.XLU[:]), "BROW4 XLU", "U2")
    act(T.U[:, 512:1024], T.U[:, 0:512].indirect(T.XLU[:]), "U0 XLU", "U1")
    ts(T.Z3[:], T.PL[:, 320:336], 0.0625, 256.0, A.mult, A.add, "PL", "Z3")
    dma("D", T.yn[:], T.Z3[:], "Z3", "yn", "o_yn")
    ts(T.BL[:], T.PL[:, 128:160], 0.0625, 256.0, A.mult, A.add, "PL", "BL")
    conv(T.PL[:, 256:288], T.U, 1024, 32, "U2", "PL")
    conv(T.PL[:, 192:224], T.U, 0, 32, "U0", "PL")
    conv(T.PL[:, 224:256], T.U, 512, 32, "U1", "PL")
    ts(T.B1[:], T.PL[:, 192:224], 0.5, None, A.is_gt, None, "PL", "B1")
    ts(T.B2[:], T.PL[:, 224:256], 0.5, None, A.is_gt, None, "PL", "B2")
    ts(T.B3[:], T.PL[:, 256:288], 0.0625, 256.0, A.mult, A.add, "PL", "B3")
    tt(T.B1[:], T.B1[:], T.B2[:], A.mult, "B1 B2", "B1")
    tt(T.B3[:], T.B3[:], T.BL[:], A.subtract, "B3 BL", "B3")
    tt(T.B4[:], T.B3[:], T.B1[:], A.mult, "B3 B1", "B4")
    tt(T.YB[:], T.BL[:], T.B4[:], A.add, "BL B4", "YB")
    dma("D", T.yb[:], T.YB[:], "YB", "yb", "o_yb")
    for q in ("V", "S", "P", "G"):
        g.wait_ge(T.sem["q" + q], cnt[q])
    for n in ("yc", "yb", "yf", "yn"):
        g.wait_ge(T.sem["o_" + n], 16)
    g.wait_ge(T.sem.loc, nloc[0])
